import numpy as np
import ml_dtypes


def mxq(x, axis, fmt="e4m3"):
    dtype, down = {"e4m3": (ml_dtypes.float8_e4m3fn, 7), "e5m2": (ml_dtypes.float8_e5m2, 14)}[fmt]
    v = np.moveaxis(np.asarray(x, np.float32).astype(ml_dtypes.bfloat16).astype(np.float64), axis, -1)
    blocks = v.reshape(v.shape[:-1] + (-1, 32))
    amax = np.abs(blocks).max(-1, keepdims=True)
    byte = np.maximum(np.where(amax > 0, np.frexp(amax)[1] - 1 + 127, 0) - down, 1)
    scale = np.exp2(byte - 127.0)
    codes = (blocks / scale).astype(np.float32).astype(dtype).astype(np.float64)
    return np.moveaxis((codes * scale).reshape(v.shape), -1, axis)


WIDE = False


def mx_kscale(k):
    if not WIDE:
        return np.ones(k)
    levels = np.array([10, -10, 5, -5, 0])
    if k % 512:
        return np.exp2(np.random.permutation(np.resize(levels, k // 32))).repeat(32)
    a = np.empty((k // 512, 16))
    for p in range(k // 512):
        a[p, :8] = np.random.permutation(np.resize(levels, 8))
        for g in range(8):
            far = levels[np.abs(levels - a[p, g]) >= 10]
            a[p, g + 8] = far[np.random.randint(len(far))]
    return np.exp2(a.ravel()).repeat(32)


def f64(x):
    return np.asarray(x).astype(np.float64)


def striped(idx):
    return np.tile(idx.reshape(-1, 16).T, (8, 1)).astype(np.uint16)


def unstriped(offs):
    return offs[:16].T.reshape(-1).astype(np.int64)


E2M1 = np.array([0.0, 0.5, 1.0, 1.5, 2.0, 3.0, 4.0, 6.0, -0.0, -0.5, -1.0, -1.5, -2.0, -3.0, -4.0, -6.0])


def pack_weight(w, fmt):
    k, n = w.shape
    w = f64(np.asarray(w, np.float32).astype(ml_dtypes.bfloat16)).reshape(k // 32, 32, n)
    amax = np.abs(w).max(1)
    if fmt == "e4m3":
        byte = np.frexp(amax)[1] - 1 + 127 - 7
    else:
        mant, ex = np.frexp(amax / 6.0)
        byte = np.where(mant > 0.5, ex, ex - 1) + 127
    byte = np.clip(np.where(amax > 0, byte, 1), 1, 254)
    scaled = (w * np.exp2(127.0 - byte)[:, None, :]).reshape(k, n).astype(np.float32)
    by_word = np.ascontiguousarray(scaled.reshape(k // 512, 128, 4, n).transpose(0, 1, 3, 2))
    if fmt == "e4m3":
        words = by_word.astype(ml_dtypes.float8_e4m3fn).view(np.uint8)
    else:
        c = by_word.astype(ml_dtypes.float4_e2m1fn).view(np.uint8) & 0xF
        words = (c[..., 0::2] | (c[..., 1::2] << 4)).reshape(k // 512, 128, 2 * n)
    return np.ascontiguousarray(words), np.ascontiguousarray(byte.astype(np.uint8).reshape(k // 512, 16, n))


def unpack_weight(words, scales, fmt):
    g, _, n = scales.shape
    words = np.ascontiguousarray(words).reshape(g, 128, n, -1)
    if fmt == "e4m3":
        vals = words.view(ml_dtypes.float8_e4m3fn).astype(np.float64)
    else:
        nib = np.empty((g, 128, n, 4), np.uint8)
        nib[..., 0::2] = words & 0xF
        nib[..., 1::2] = words >> 4
        vals = E2M1[nib]
    vals = vals * np.repeat(np.exp2(scales.astype(np.float64) - 127.0), 8, axis=1)[..., None]
    return vals.transpose(0, 1, 3, 2).reshape(g * 512, n)


def gelu(v):
    return 0.5 * v * (1.0 + np.tanh(np.sqrt(2.0 / np.pi) * (v + 0.044715 * v**3)))


def striped8(idx):
    return np.concatenate([v.reshape(-1, 16).T for v in idx]).astype(np.uint16)


def unstriped8(offs):
    return np.stack([offs[16 * g:16 * g + 16].T.reshape(-1) for g in range(8)]).astype(np.int64)


def runs(v, idx8):
    k = np.arange(v.shape[0])
    return v[k[:, None], idx8[k % 512 // 64]]


K, T, S, H, M = 1024, 2048, 1024, 768, 512

def setup_inputs():
    n = np.random.standard_normal
    s = mx_kscale(K)[:, None]
    w = mx_kscale(S)[:, None]
    tab_words, tab_scales = pack_weight(n((K, T)) * s, "e4m3")
    offs = striped8(np.stack([np.random.permutation(T)[:S] for _ in range(8)]))
    w1_words, w1_scales = pack_weight(n((K, H)) / np.sqrt(K) / s, "e2m1")
    w2 = (n((K, H)) / np.sqrt(K) / s).astype(np.float32)
    left = np.exp(0.3 * n(H)).astype(np.float32)
    flow = (np.exp(0.3 * n(S)) * w[:, 0]).astype(np.float32)
    regrid = (n((S, M)) / np.sqrt(S) / w).astype(np.float32)
    bias = (0.5 * n(H)).astype(np.float32)
    return {"tab_words": tab_words, "tab_scales": tab_scales, "offs": offs,
            "w1_words": w1_words, "w1_scales": w1_scales, "w2": w2,
            "left": left, "flow": flow, "regrid": regrid, "bias": bias}

def reference(tab_words, tab_scales, offs, w1_words, w1_scales, w2, left, flow, regrid, bias):
    v = runs(unpack_weight(tab_words, tab_scales, "e4m3"), unstriped8(offs))
    w1 = unpack_weight(w1_words, w1_scales, "e2m1")
    a = v.T @ w1
    b = v.T @ mxq(f64(w2), 0, "e4m3")
    h = np.abs(a) * b * f64(left)[None, :]
    h = h * f64(flow)[:, None]
    y = mxq(h, 0, "e4m3").T @ mxq(f64(regrid), 0, "e4m3")
    return y + f64(bias)[:, None]

@@ -1,0 +1,318 @@
+from contextlib import ExitStack
+
+import concourse.mybir as mybir
+from concourse.masks import make_identity
+
+K, T, S, H, M = 1024, 2048, 1024, 768, 512
+FLOPS = 2 * 2 * K * S * H + 2 * S * H * M
+
+F32 = mybir.dt.float32
+BF16 = mybir.dt.bfloat16
+I32 = mybir.dt.int32
+U32 = mybir.dt.uint32
+U16 = mybir.dt.uint16
+U8 = mybir.dt.uint8
+FP8X4 = mybir.dt.float8_e4m3fn_x4
+FP4X4 = mybir.dt.float4_e2m1fn_x4
+MULT = mybir.AluOpType.mult
+ACT = mybir.ActivationFunctionType
+
+P = 128
+PACK = 4
+PASS = P * PACK
+K_PASSES = K // PASS
+J_PASSES = S // PASS
+CHUNK = 256
+CHUNKS = H // CHUNK
+R_TILES = H // P
+LIST_COLS = PASS // 16
+
+
+def tile_list_flowline_velocity_regrid_kernel(
+    tc, tab_words, tab_scales, offs, w1_words, w1_scales, w2, left, flow, regrid, bias, out
+):
+    nc = tc.nc
+    with ExitStack() as ctx:
+        keep = ctx.enter_context(tc.tile_pool(name="keep", bufs=1))
+        ring = ctx.enter_context(tc.tile_pool(name="ring", bufs=3))
+        psum_ab = ctx.enter_context(tc.psum_pool(name="psum_ab", bufs=3))
+        psum_out = ctx.enter_context(tc.psum_pool(name="psum_out", bufs=2))
+
+        def kept(shape, dtype, name, tag=None):
+            return keep.tile(shape, dtype, name=name, tag=tag or name, align_bytes=64)
+
+        offsets = keep.tile([P, S // 16], U16, name="offsets")
+        nc.sync.dma_start(offsets[:], offs)
+
+        scale_window = kept([P, T], U8, "scale_window")
+        nc.gpsimd.memset(scale_window[:].bitcast(I32), 0)
+        identity = kept([P, P], F32, "identity")
+        make_identity(nc, identity[:])
+        v_plane1 = kept([P, S], U8, "v_plane1")
+        nc.gpsimd.memset(v_plane1[:].bitcast(I32), 0)
+        w1_plane = kept([P, K_PASSES, H], U8, "w1_plane")
+        nc.gpsimd.memset(w1_plane[:].rearrange("p a n -> p (a n)").bitcast(I32), 0)
+
+
+        word_window = [kept([P, T], I32, f"word_window{a}") for a in range(K_PASSES)]
+        w2_raw = {}
+
+        def load_words(a):
+            nc.sync.dma_start(word_window[a][:], tab_words[a].rearrange("p t i -> p (t i)").bitcast(I32))
+
+        def load_w2(a, c, tag=None):
+            w2_raw[a, c] = kept([P, PACK, CHUNK], F32, f"w2_raw{a}{c}", tag)
+            rows = w2[a * PASS : (a + 1) * PASS, c * CHUNK : (c + 1) * CHUNK]
+            nc.sync.dma_start(w2_raw[a, c][:], rows.rearrange("(p i) n -> p i n", i=PACK))
+
+        regrid_raw = {}
+
+        def load_regrid(g, tag):
+            regrid_raw[g] = kept([P, PACK, M], F32, f"regrid_raw{g}", tag)
+            rows = regrid[g * PASS : (g + 1) * PASS, :]
+            nc.sync.dma_start(regrid_raw[g][:], rows.rearrange("(p t) m -> p t m", t=PACK))
+
+        load_words(0)
+        for a in range(K_PASSES):
+            for c in range(2):
+                nc.scalar.dma_start(
+                    scale_window[:].bitcast(I32)[4 * a + c : P : 16, :],
+                    tab_scales[a, c::2, :].bitcast(I32),
+                )
+        load_w2(0, 0)
+        load_words(1)
+
+        left_cols = kept([P, R_TILES], F32, "left_cols")
+        flow_cols = kept([P, J_PASSES, PACK], F32, "flow_cols")
+        with nc.allow_non_contiguous_dma(reason="one value of a vector to each partition"):
+            nc.scalar.dma_start(left_cols[:], left.rearrange("(c p) -> p c", p=P))
+        load_w2(1, 0)
+        w1_codes = kept([P, K_PASSES, 2 * H], U8, "w1_codes")
+        nc.sync.dma_start(w1_codes[:].bitcast(I32), w1_words.rearrange("a p n -> p a n").bitcast(I32))
+        for q in range(4):
+            nc.gpsimd.dma_start(
+                w1_plane[32 * q : 32 * q + 4, :, :].bitcast(I32),
+                w1_scales[:, 4 * q : 4 * q + 4, :].rearrange("a r n -> r a n").bitcast(I32),
+            )
+        nc.sync.dma_start(flow_cols[:], flow.rearrange("(g p t) -> p g t", p=P, t=PACK))
+
+        left_rows = kept([P, H], F32, "left_rows")
+        for first in range(0, R_TILES, 4):
+            count = min(4, R_TILES - first)
+            spread = psum_out.tile([P, M], F32, name="acc")
+            for c in range(count):
+                column = left_cols[:, first + c : first + c + 1].to_broadcast([P, P])
+                nc.tensor.transpose(spread[:, c * P : (c + 1) * P], column, identity[:])
+            nc.scalar.activation(left_rows[:, first * P : (first + count) * P], spread[:, : count * P], ACT.Copy)
+
+        scale_picked = kept([P, S], U8, "scale_picked")
+        nc.vector.tensor_copy(scale_picked[:], scale_window[:].indirect(offsets[:]))
+        v_plane0 = kept([P, S], U8, "v_plane0")
+        nc.vector.tensor_copy(
+            v_plane0[:].rearrange("k (g t p) -> k g t p", g=J_PASSES, t=PACK),
+            scale_picked[:].rearrange("k (g p t) -> k g t p", g=J_PASSES, t=PACK),
+        )
+        rows0 = v_plane0[:].bitcast(I32)
+        rows1 = v_plane1[:].bitcast(I32)
+        for c in range(2):
+            nc.scalar.dma_start(rows0[2 + c : P : 32, :], rows0[16 + c : P : 32, :])
+        for r in range(4):
+            nc.scalar.dma_start(rows1[r:P:32, :], rows0[16 * (r // 2) + 4 + r % 2 : P : 32, :])
+        v_plane = [v_plane0, v_plane1]
+
+        words_picked = {}
+        v_codes = {}
+
+        def gather_words(a, g):
+            words_picked[a, g] = kept([P, PASS], U32, f"words_picked{a}{g}")
+            window = word_window[a][:].bitcast(U32)
+            nc.vector.tensor_copy(
+                words_picked[a, g][:], window.indirect(offsets[:, g * LIST_COLS : (g + 1) * LIST_COLS])
+            )
+
+        def order_words(a, g):
+            v_codes[a, g] = kept([P, PACK, P], I32, f"v_codes{a}{g}")
+            nc.vector.tensor_copy(
+                v_codes[a, g][:].rearrange("k t (c i) -> k c t i", i=4),
+                words_picked[a, g][:].bitcast(I32).rearrange("k (c i t) -> k c t i", i=4, t=PACK),
+            )
+
+        def round_and_interleave(raw, width, name):
+            grouped = kept([P, width, PACK], BF16, name)
+            nc.scalar.copy(
+                grouped[:].rearrange("p (c i) t -> p c t i", i=4),
+                raw[:].rearrange("p t (c i) -> p c t i", i=4),
+            )
+            return grouped
+
+        def quantise(grouped, codes, plane):
+            nc.vector.quantize_mx(out=codes.bitcast(FP8X4), scales=plane, in_=grouped.rearrange("p n t -> p (n t)"))
+
+        w2_grouped, w2_codes, w2_plane = {}, {}, {}
+
+        def round_w2(a, c):
+            w2_grouped[a, c] = round_and_interleave(w2_raw[a, c], CHUNK, f"w2_grouped{a}{c}")
+
+        def quantise_w2(a, c):
+            w2_codes[a, c] = kept([P, CHUNK], U32, f"w2_codes{a}{c}")
+            w2_plane[a, c] = kept([P, CHUNK], U8, f"w2_plane{a}{c}")
+            quantise(w2_grouped[a, c][:], w2_codes[a, c][:], w2_plane[a, c][:])
+
+        regrid_grouped, regrid_codes, regrid_plane = {}, {}, {}
+
+        def round_regrid(g):
+            regrid_grouped[g] = round_and_interleave(regrid_raw[g], M, f"regrid_grouped{g}")
+
+        def quantise_regrid(g):
+            regrid_codes[g] = kept([P, M], U32, f"regrid_codes{g}")
+            regrid_plane[g] = kept([P, M], U8, f"regrid_plane{g}")
+            quantise(regrid_grouped[g][:], regrid_codes[g][:], regrid_plane[g][:])
+
+        size_a, weighted_b, h_grouped, h_codes, h_plane = {}, {}, {}, {}, {}
+
+        def first_products(c, g, pair):
+            if pair == 0:
+                size_a[c, g] = ring.tile([P, PACK, CHUNK], F32, name="size_a")
+                weighted_b[c, g] = ring.tile([P, PACK, CHUNK], F32, name="weighted_b")
+            bank_a = psum_ab.tile([P, 2, CHUNK], F32, name="bank_a")
+            bank_b = psum_ab.tile([P, 2, CHUNK], F32, name="bank_b")
+            for u in range(2):
+                t = 2 * pair + u
+                j_cols = slice(g * PASS + t * P, g * PASS + (t + 1) * P)
+                for a in range(K_PASSES):
+                    nc.tensor.matmul_mx(
+                        out=bank_b[:, u, :],
+                        lhsT=v_codes[a, g][:, t, :].bitcast(FP8X4),
+                        lhsT_scale=v_plane[a][:, j_cols],
+                        rhs=w2_codes[a, c][:].bitcast(FP8X4),
+                        rhs_scale=w2_plane[a, c][:],
+                        start=(a == 0),
+                        stop=(a == K_PASSES - 1),
+                    )
+                for half in range(CHUNK // P):
+                    r0 = c * CHUNK + half * P
+                    for a in range(K_PASSES):
+                        nc.tensor.matmul_mx(
+                            out=bank_a[:, u, half * P : (half + 1) * P],
+                            lhsT=v_codes[a, g][:, t, :].bitcast(FP8X4),
+                            lhsT_scale=v_plane[a][:, j_cols],
+                            rhs=w1_codes[:, a, 2 * r0 : 2 * (r0 + P)].bitcast(FP4X4),
+                            rhs_scale=w1_plane[:, a, r0 : r0 + P],
+                            start=(a == 0),
+                            stop=(a == K_PASSES - 1),
+                        )
+            nc.scalar.activation(size_a[c, g][:, 2 * pair : 2 * pair + 2, :], bank_a[:], ACT.Abs)
+            for u in range(2):
+                t = 2 * pair + u
+                nc.vector.scalar_tensor_tensor(
+                    out=weighted_b[c, g][:, t, :],
+                    in0=bank_b[:, u, :],
+                    scalar=flow_cols[:, g, t : t + 1],
+                    in1=left_rows[:, c * CHUNK : (c + 1) * CHUNK],
+                    op0=MULT,
+                    op1=MULT,
+                )
+
+        def make_h(c, g, cols):
+            if cols.start == 0:
+                h_grouped[c, g] = ring.tile([P, CHUNK, PACK], BF16, name="h_grouped", align_bytes=64)
+            nc.vector.tensor_tensor(
+                h_grouped[c, g][:, cols, :].rearrange("p (c i) t -> p c t i", i=2),
+                weighted_b[c, g][:, :, cols].rearrange("p t (c i) -> p c t i", i=2),
+                size_a[c, g][:, :, cols].rearrange("p t (c i) -> p c t i", i=2),
+                MULT,
+            )
+
+        def quantise_h(c, g, cols):
+            if cols.start == 0:
+                h_codes[c, g] = kept([P, CHUNK], U32, f"h_codes{c}{g}")
+                h_plane[c, g] = kept([P, CHUNK], U8, f"h_plane{c}{g}")
+            quantise(h_grouped[c, g][:, cols, :], h_codes[c, g][:, cols], h_plane[c, g][:, cols])
+
+        def second_product(c, half):
+            cols = slice(half * P, (half + 1) * P)
+            r_tile = c * (CHUNK // P) + half
+            acc = psum_out.tile([P, M], F32, name="acc")
+            for g in range(J_PASSES):
+                nc.tensor.matmul_mx(
+                    out=acc[:],
+                    lhsT=h_codes[c, g][:, cols].bitcast(FP8X4),
+                    lhsT_scale=h_plane[c, g][:, cols],
+                    rhs=regrid_codes[g][:].bitcast(FP8X4),
+                    rhs_scale=regrid_plane[g][:],
+                    start=(g == 0),
+                    stop=(g == J_PASSES - 1),
+                )
+            result = ring.tile([P, M], F32, name="result")
+            nc.scalar.activation(result[:], acc[:], ACT.Identity, bias=bias_cols[:, r_tile : r_tile + 1])
+            nc.sync.dma_start(out[r_tile * P : (r_tile + 1) * P, :], result[:])
+
+        load_w2(0, 1, "scale_picked")
+        round_w2(0, 0)
+        load_w2(1, 1, "w2_raw00")
+        gather_words(0, 0)
+        gather_words(0, 1)
+        order_words(0, 0)
+        load_regrid(0, "words_picked00")
+        quantise_w2(0, 0)
+        gather_words(1, 0)
+        round_w2(1, 0)
+        order_words(0, 1)
+        load_regrid(1, "words_picked01")
+        order_words(1, 0)
+        load_w2(0, 2, "words_picked10")
+        load_w2(1, 2, "w2_raw10")
+        quantise_w2(1, 0)
+        gather_words(1, 1)
+        round_w2(0, 1)
+        order_words(1, 1)
+        bias_cols = kept([P, R_TILES], F32, "bias_cols", "words_picked11")
+        with nc.allow_non_contiguous_dma(reason="one value of a vector to each partition"):
+            nc.sync.dma_start(bias_cols[:], bias.rearrange("(c p) -> p c", p=P))
+
+        whole = slice(0, CHUNK)
+        halves = [slice(0, P), slice(P, CHUNK)]
+
+        first_products(0, 0, 0)
+        round_w2(1, 1)
+        first_products(0, 0, 1)
+        quantise_w2(0, 1)
+        first_products(0, 1, 0)
+        make_h(0, 0, whole)
+        quantise_w2(1, 1)
+        round_regrid(0)
+        first_products(0, 1, 1)
+        quantise_h(0, 0, whole)
+        first_products(1, 0, 0)
+        make_h(0, 1, whole)
+        quantise_regrid(0)
+        round_regrid(1)
+        first_products(1, 0, 1)
+        quantise_h(0, 1, whole)
+        round_w2(0, 2)
+        first_products(1, 1, 0)
+        make_h(1, 0, whole)
+        quantise_regrid(1)
+        round_w2(1, 2)
+        first_products(1, 1, 1)
+        quantise_w2(0, 2)
+        quantise_h(1, 0, whole)
+        quantise_w2(1, 2)
+        second_product(0, 0)
+        second_product(0, 1)
+        first_products(2, 0, 0)
+        make_h(1, 1, whole)
+        first_products(2, 0, 1)
+        quantise_h(1, 1, whole)
+        first_products(2, 1, 0)
+        second_product(1, 0)
+        second_product(1, 1)
+        make_h(2, 0, whole)
+        first_products(2, 1, 1)
+        quantise_h(2, 0, whole)
+        make_h(2, 1, halves[0])
+        make_h(2, 1, halves[1])
+        quantise_h(2, 1, halves[0])
+        quantise_h(2, 1, halves[1])
+        second_product(2, 0)
+        second_product(2, 1)

@@ -22,8 +22,8 @@ PACK = 4
 PASS = P * PACK
 K_PASSES = K // PASS
 J_PASSES = S // PASS
-CHUNK = 256
-CHUNKS = H // CHUNK
+BANK = 512
+CHUNKS = ((0, 256), (256, 512))
 R_TILES = H // P
 LIST_COLS = PASS // 16
 
@@ -45,27 +45,24 @@ def tile_list_flowline_velocity_regrid_kernel(
         nc.sync.dma_start(offsets[:], offs)
 
         scale_window = kept([P, T], U8, "scale_window")
-        nc.gpsimd.memset(scale_window[:].bitcast(I32), 0)
+        nc.vector.memset(scale_window[:].bitcast(I32), 0)
+        w1_plane = kept([P, K_PASSES, H], U8, "w1_plane")
+        nc.vector.memset(w1_plane[:].rearrange("p a n -> p (a n)").bitcast(I32), 0)
+        v_plane = kept([P, K_PASSES * S], U8, "v_plane")
+        nc.vector.memset(v_plane[:].bitcast(I32), 0)
         identity = kept([P, P], F32, "identity")
         make_identity(nc, identity[:])
-        v_plane1 = kept([P, S], U8, "v_plane1")
-        nc.gpsimd.memset(v_plane1[:].bitcast(I32), 0)
-        w1_plane = kept([P, K_PASSES, H], U8, "w1_plane")
-        nc.gpsimd.memset(w1_plane[:].rearrange("p a n -> p (a n)").bitcast(I32), 0)
-
 
         word_window = [kept([P, T], I32, f"word_window{a}") for a in range(K_PASSES)]
-        w2_raw = {}
+        w2_raw, regrid_raw = {}, {}
 
         def load_words(a):
             nc.sync.dma_start(word_window[a][:], tab_words[a].rearrange("p t i -> p (t i)").bitcast(I32))
 
-        def load_w2(a, c, tag=None):
-            w2_raw[a, c] = kept([P, PACK, CHUNK], F32, f"w2_raw{a}{c}", tag)
-            rows = w2[a * PASS : (a + 1) * PASS, c * CHUNK : (c + 1) * CHUNK]
-            nc.sync.dma_start(w2_raw[a, c][:], rows.rearrange("(p i) n -> p i n", i=PACK))
-
-        regrid_raw = {}
+        def load_w2(a, first, width, tag=None):
+            w2_raw[a, first] = kept([P, PACK, width], F32, f"w2_raw{a}_{first}", tag)
+            rows = w2[a * PASS : (a + 1) * PASS, first : first + width]
+            nc.sync.dma_start(w2_raw[a, first][:], rows.rearrange("(p i) n -> p i n", i=PACK))
 
         def load_regrid(g, tag):
             regrid_raw[g] = kept([P, PACK, M], F32, f"regrid_raw{g}", tag)
@@ -74,27 +71,23 @@ def tile_list_flowline_velocity_regrid_kernel(
 
         load_words(0)
         for a in range(K_PASSES):
-            for c in range(2):
-                nc.scalar.dma_start(
-                    scale_window[:].bitcast(I32)[4 * a + c : P : 16, :],
-                    tab_scales[a, c::2, :].bitcast(I32),
-                )
-        load_w2(0, 0)
+            nc.scalar.dma_start(scale_window[:].bitcast(I32)[a:P:8, :], tab_scales[a].bitcast(I32))
+        load_w2(0, 0, 256)
+        load_w2(1, 0, 256)
+        load_w2(1, 256, 256)
         load_words(1)
 
         left_cols = kept([P, R_TILES], F32, "left_cols")
-        flow_cols = kept([P, J_PASSES, PACK], F32, "flow_cols")
         with nc.allow_non_contiguous_dma(reason="one value of a vector to each partition"):
             nc.scalar.dma_start(left_cols[:], left.rearrange("(c p) -> p c", p=P))
-        load_w2(1, 0)
         w1_codes = kept([P, K_PASSES, 2 * H], U8, "w1_codes")
         nc.sync.dma_start(w1_codes[:].bitcast(I32), w1_words.rearrange("a p n -> p a n").bitcast(I32))
+        load_w2(1, 512, 256)
         for q in range(4):
             nc.gpsimd.dma_start(
                 w1_plane[32 * q : 32 * q + 4, :, :].bitcast(I32),
                 w1_scales[:, 4 * q : 4 * q + 4, :].rearrange("a r n -> r a n").bitcast(I32),
             )
-        nc.sync.dma_start(flow_cols[:], flow.rearrange("(g p t) -> p g t", p=P, t=PACK))
 
         left_rows = kept([P, H], F32, "left_rows")
         for first in range(0, R_TILES, 4):
@@ -105,117 +98,132 @@ def tile_list_flowline_velocity_regrid_kernel(
                 nc.tensor.transpose(spread[:, c * P : (c + 1) * P], column, identity[:])
             nc.scalar.activation(left_rows[:, first * P : (first + count) * P], spread[:, : count * P], ACT.Copy)
 
+        flow_cols = kept([P, J_PASSES, PACK], F32, "flow_cols", "left_cols")
+        nc.sync.dma_start(flow_cols[:], flow.rearrange("(g p t) -> p g t", p=P, t=PACK))
+
         scale_picked = kept([P, S], U8, "scale_picked")
-        nc.vector.tensor_copy(scale_picked[:], scale_window[:].indirect(offsets[:]))
-        v_plane0 = kept([P, S], U8, "v_plane0")
-        nc.vector.tensor_copy(
-            v_plane0[:].rearrange("k (g t p) -> k g t p", g=J_PASSES, t=PACK),
-            scale_picked[:].rearrange("k (g p t) -> k g t p", g=J_PASSES, t=PACK),
-        )
-        rows0 = v_plane0[:].bitcast(I32)
-        rows1 = v_plane1[:].bitcast(I32)
-        for c in range(2):
-            nc.scalar.dma_start(rows0[2 + c : P : 32, :], rows0[16 + c : P : 32, :])
-        for r in range(4):
-            nc.scalar.dma_start(rows1[r:P:32, :], rows0[16 * (r // 2) + 4 + r % 2 : P : 32, :])
-        v_plane = [v_plane0, v_plane1]
 
-        words_picked = {}
-        v_codes = {}
+        def gather_scales():
+            scale_ordered = kept([P, S], U8, "scale_ordered")
+            nc.vector.tensor_copy(scale_picked[:], scale_window[:].indirect(offsets[:]))
+            nc.vector.tensor_copy(
+                scale_ordered[:].rearrange("k (g t p) -> k g t p", g=J_PASSES, t=PACK),
+                scale_picked[:].rearrange("k (g p t) -> k g t p", g=J_PASSES, t=PACK),
+            )
+            source = scale_ordered[:].bitcast(I32)
+            target = v_plane[:].bitcast(I32)
+            for a in range(K_PASSES):
+                for q in range(4):
+                    queue = nc.gpsimd if q == 0 else nc.sync
+                    queue.dma_start(
+                        target[32 * q : 32 * q + 4, a * S // 4 : (a + 1) * S // 4],
+                        source[32 * q + a : 32 * (q + 1) : 8, :],
+                    )
 
-        def gather_words(a, g):
-            words_picked[a, g] = kept([P, PASS], U32, f"words_picked{a}{g}")
+        words_picked = kept([P, K_PASSES, S], U32, "words_picked")
+        v_codes = [kept([P, K_PASSES, PACK, P], I32, f"v_codes{g}") for g in range(J_PASSES)]
+
+        def gather_words(a, g, count):
             window = word_window[a][:].bitcast(U32)
             nc.vector.tensor_copy(
-                words_picked[a, g][:], window.indirect(offsets[:, g * LIST_COLS : (g + 1) * LIST_COLS])
+                words_picked[:, a, g * PASS : (g + count) * PASS],
+                window.indirect(offsets[:, g * LIST_COLS : (g + count) * LIST_COLS]),
             )
 
-        def order_words(a, g):
-            v_codes[a, g] = kept([P, PACK, P], I32, f"v_codes{a}{g}")
+        def order_words(g):
+            picked = words_picked[:, :, g * PASS : (g + 1) * PASS].bitcast(I32)
             nc.vector.tensor_copy(
-                v_codes[a, g][:].rearrange("k t (c i) -> k c t i", i=4),
-                words_picked[a, g][:].bitcast(I32).rearrange("k (c i t) -> k c t i", i=4, t=PACK),
+                v_codes[g][:].rearrange("k a t (c i) -> k a c t i", i=4),
+                picked.rearrange("k a (c i t) -> k a c t i", i=4, t=PACK),
             )
 
-        def round_and_interleave(raw, width, name):
-            grouped = kept([P, width, PACK], BF16, name)
+        def round_and_interleave(grouped, raw):
             nc.scalar.copy(
-                grouped[:].rearrange("p (c i) t -> p c t i", i=4),
-                raw[:].rearrange("p t (c i) -> p c t i", i=4),
+                grouped.rearrange("p (c i) t -> p c t i", i=4),
+                raw.rearrange("p t (c i) -> p c t i", i=4),
             )
-            return grouped
 
         def quantise(grouped, codes, plane):
             nc.vector.quantize_mx(out=codes.bitcast(FP8X4), scales=plane, in_=grouped.rearrange("p n t -> p (n t)"))
 
         w2_grouped, w2_codes, w2_plane = {}, {}, {}
+        for a in range(K_PASSES):
+            for c, (first, width) in enumerate(CHUNKS):
+                w2_grouped[a, c] = kept([P, width, PACK], BF16, f"w2_grouped{a}{c}")
+                w2_codes[a, c] = kept([P, width], U32, f"w2_codes{a}{c}")
+                w2_plane[a, c] = kept([P, width], U8, f"w2_plane{a}{c}")
 
-        def round_w2(a, c):
-            w2_grouped[a, c] = round_and_interleave(w2_raw[a, c], CHUNK, f"w2_grouped{a}{c}")
+        def round_w2(a, c, first):
+            raw = w2_raw[a, first]
+            start = first - CHUNKS[c][0]
+            round_and_interleave(w2_grouped[a, c][:, start : start + raw.shape[2], :], raw[:])
 
         def quantise_w2(a, c):
-            w2_codes[a, c] = kept([P, CHUNK], U32, f"w2_codes{a}{c}")
-            w2_plane[a, c] = kept([P, CHUNK], U8, f"w2_plane{a}{c}")
             quantise(w2_grouped[a, c][:], w2_codes[a, c][:], w2_plane[a, c][:])
 
-        regrid_grouped, regrid_codes, regrid_plane = {}, {}, {}
+        regrid_grouped = [kept([P, M, PACK], BF16, f"regrid_grouped{g}") for g in range(J_PASSES)]
+        regrid_codes = [kept([P, M], U32, f"regrid_codes{g}") for g in range(J_PASSES)]
+        regrid_plane = [kept([P, M], U8, f"regrid_plane{g}") for g in range(J_PASSES)]
 
         def round_regrid(g):
-            regrid_grouped[g] = round_and_interleave(regrid_raw[g], M, f"regrid_grouped{g}")
+            round_and_interleave(regrid_grouped[g][:], regrid_raw[g][:])
 
         def quantise_regrid(g):
-            regrid_codes[g] = kept([P, M], U32, f"regrid_codes{g}")
-            regrid_plane[g] = kept([P, M], U8, f"regrid_plane{g}")
             quantise(regrid_grouped[g][:], regrid_codes[g][:], regrid_plane[g][:])
 
         size_a, weighted_b, h_grouped, h_codes, h_plane = {}, {}, {}, {}, {}
+        for c, (first, width) in enumerate(CHUNKS):
+            for g in range(J_PASSES):
+                size_a[c, g] = kept([P, PACK, width], F32, f"size_a{c}{g}")
+                weighted_b[c, g] = kept([P, PACK, width], F32, f"weighted_b{c}{g}")
+                h_grouped[c, g] = kept([P, width, PACK], BF16, f"h_grouped{c}{g}")
+                h_codes[c, g] = kept([P, width], U32, f"h_codes{c}{g}")
+                h_plane[c, g] = kept([P, width], U8, f"h_plane{c}{g}")
 
-        def first_products(c, g, pair):
-            if pair == 0:
-                size_a[c, g] = ring.tile([P, PACK, CHUNK], F32, name="size_a")
-                weighted_b[c, g] = ring.tile([P, PACK, CHUNK], F32, name="weighted_b")
-            bank_a = psum_ab.tile([P, 2, CHUNK], F32, name="bank_a")
-            bank_b = psum_ab.tile([P, 2, CHUNK], F32, name="bank_b")
-            for u in range(2):
-                t = 2 * pair + u
-                j_cols = slice(g * PASS + t * P, g * PASS + (t + 1) * P)
+        def first_products(c, g, t0):
+            first, width = CHUNKS[c]
+            slots = BANK // width
+            step = BANK if width == BANK else P
+            bank_a = psum_ab.tile([P, slots, width], F32, name="bank_a")
+            bank_b = psum_ab.tile([P, slots, width], F32, name="bank_b")
+            for u in range(slots):
+                t = t0 + u
+                j0 = g * PASS + t * P
                 for a in range(K_PASSES):
                     nc.tensor.matmul_mx(
                         out=bank_b[:, u, :],
-                        lhsT=v_codes[a, g][:, t, :].bitcast(FP8X4),
-                        lhsT_scale=v_plane[a][:, j_cols],
+                        lhsT=v_codes[g][:, a, t, :].bitcast(FP8X4),
+                        lhsT_scale=v_plane[:, a * S + j0 : a * S + j0 + P],
                         rhs=w2_codes[a, c][:].bitcast(FP8X4),
                         rhs_scale=w2_plane[a, c][:],
                         start=(a == 0),
                         stop=(a == K_PASSES - 1),
                     )
-                for half in range(CHUNK // P):
-                    r0 = c * CHUNK + half * P
+                for n0 in range(0, width, step):
+                    r0 = first + n0
                     for a in range(K_PASSES):
                         nc.tensor.matmul_mx(
-                            out=bank_a[:, u, half * P : (half + 1) * P],
-                            lhsT=v_codes[a, g][:, t, :].bitcast(FP8X4),
-                            lhsT_scale=v_plane[a][:, j_cols],
-                            rhs=w1_codes[:, a, 2 * r0 : 2 * (r0 + P)].bitcast(FP4X4),
-                            rhs_scale=w1_plane[:, a, r0 : r0 + P],
+                            out=bank_a[:, u, n0 : n0 + step],
+                            lhsT=v_codes[g][:, a, t, :].bitcast(FP8X4),
+                            lhsT_scale=v_plane[:, a * S + j0 : a * S + j0 + P],
+                            rhs=w1_codes[:, a, 2 * r0 : 2 * (r0 + step)].bitcast(FP4X4),
+                            rhs_scale=w1_plane[:, a, r0 : r0 + step],
                             start=(a == 0),
                             stop=(a == K_PASSES - 1),
                         )
-            nc.scalar.activation(size_a[c, g][:, 2 * pair : 2 * pair + 2, :], bank_a[:], ACT.Abs)
-            for u in range(2):
-                t = 2 * pair + u
+            nc.scalar.activation(size_a[c, g][:, t0 : t0 + slots, :], bank_a[:], ACT.Abs)
+            for u in range(slots):
+                t = t0 + u
                 nc.vector.scalar_tensor_tensor(
                     out=weighted_b[c, g][:, t, :],
                     in0=bank_b[:, u, :],
                     scalar=flow_cols[:, g, t : t + 1],
-                    in1=left_rows[:, c * CHUNK : (c + 1) * CHUNK],
+                    in1=left_rows[:, first : first + width],
                     op0=MULT,
                     op1=MULT,
                 )
 
         def make_h(c, g, cols):
-            if cols.start == 0:
-                h_grouped[c, g] = ring.tile([P, CHUNK, PACK], BF16, name="h_grouped", align_bytes=64)
             nc.vector.tensor_tensor(
                 h_grouped[c, g][:, cols, :].rearrange("p (c i) t -> p c t i", i=2),
                 weighted_b[c, g][:, :, cols].rearrange("p t (c i) -> p c t i", i=2),
@@ -224,95 +232,102 @@ def tile_list_flowline_velocity_regrid_kernel(
             )
 
         def quantise_h(c, g, cols):
-            if cols.start == 0:
-                h_codes[c, g] = kept([P, CHUNK], U32, f"h_codes{c}{g}")
-                h_plane[c, g] = kept([P, CHUNK], U8, f"h_plane{c}{g}")
             quantise(h_grouped[c, g][:, cols, :], h_codes[c, g][:, cols], h_plane[c, g][:, cols])
 
-        def second_product(c, half):
-            cols = slice(half * P, (half + 1) * P)
-            r_tile = c * (CHUNK // P) + half
-            acc = psum_out.tile([P, M], F32, name="acc")
+        def regrid_product(c, n, acc, m_cols):
+            cols = slice(n * P, (n + 1) * P)
             for g in range(J_PASSES):
                 nc.tensor.matmul_mx(
-                    out=acc[:],
+                    out=acc,
                     lhsT=h_codes[c, g][:, cols].bitcast(FP8X4),
                     lhsT_scale=h_plane[c, g][:, cols],
-                    rhs=regrid_codes[g][:].bitcast(FP8X4),
-                    rhs_scale=regrid_plane[g][:],
+                    rhs=regrid_codes[g][:, m_cols].bitcast(FP8X4),
+                    rhs_scale=regrid_plane[g][:, m_cols],
                     start=(g == 0),
                     stop=(g == J_PASSES - 1),
                 )
+
+        def second_product(c, n):
+            r_tile = CHUNKS[c][0] // P + n
+            acc = psum_out.tile([P, M], F32, name="acc")
+            regrid_product(c, n, acc[:], slice(0, M))
             result = ring.tile([P, M], F32, name="result")
             nc.scalar.activation(result[:], acc[:], ACT.Identity, bias=bias_cols[:, r_tile : r_tile + 1])
             nc.sync.dma_start(out[r_tile * P : (r_tile + 1) * P, :], result[:])
 
-        load_w2(0, 1, "scale_picked")
-        round_w2(0, 0)
-        load_w2(1, 1, "w2_raw00")
-        gather_words(0, 0)
-        gather_words(0, 1)
-        order_words(0, 0)
-        load_regrid(0, "words_picked00")
+        def last_second_product(c, n):
+            r_tile = CHUNKS[c][0] // P + n
+            rows = slice(r_tile * P, (r_tile + 1) * P)
+            low, high = slice(0, M // 2), slice(M // 2, M)
+            acc_low = psum_ab.tile([P, M // 2], F32, name="bank_a")
+            acc_high = psum_ab.tile([P, M // 2], F32, name="bank_b")
+            regrid_product(c, n, acc_low[:], low)
+            regrid_product(c, n, acc_high[:], high)
+            result_low = kept([P, M // 2], F32, "result_low")
+            result_high = kept([P, M // 2], F32, "result_high")
+            nc.vector.tensor_scalar_add(result_low[:], acc_low[:], bias_cols[:, r_tile : r_tile + 1])
+            nc.sync.dma_start(out[rows, low], result_low[:])
+            nc.scalar.activation(result_high[:], acc_high[:], ACT.Identity, bias=bias_cols[:, r_tile : r_tile + 1])
+            nc.scalar.dma_start(out[rows, high], result_high[:])
+
+        gather_words(0, 0, 2)
+        round_w2(0, 0, 0)
+        round_w2(1, 0, 0)
+        round_w2(1, 1, 256)
+        gather_scales()
+        load_w2(0, 256, 512, "scale_picked")
         quantise_w2(0, 0)
-        gather_words(1, 0)
-        round_w2(1, 0)
-        order_words(0, 1)
-        load_regrid(1, "words_picked01")
-        order_words(1, 0)
-        load_w2(0, 2, "words_picked10")
-        load_w2(1, 2, "w2_raw10")
         quantise_w2(1, 0)
-        gather_words(1, 1)
-        round_w2(0, 1)
-        order_words(1, 1)
-        bias_cols = kept([P, R_TILES], F32, "bias_cols", "words_picked11")
+        gather_words(1, 0, 1)
+        order_words(0)
+        gather_words(1, 1, 1)
+        load_regrid(0, "scale_ordered")
+        round_w2(1, 1, 512)
+        order_words(1)
+        load_regrid(1, "words_picked")
+        bias_cols = kept([P, R_TILES], F32, "bias_cols", "w2_raw1_512")
         with nc.allow_non_contiguous_dma(reason="one value of a vector to each partition"):
             nc.sync.dma_start(bias_cols[:], bias.rearrange("(c p) -> p c", p=P))
 
-        whole = slice(0, CHUNK)
-        halves = [slice(0, P), slice(P, CHUNK)]
+        narrow, wide = slice(0, 256), slice(0, 512)
+        tiles = [slice(n * P, (n + 1) * P) for n in range(4)]
 
         first_products(0, 0, 0)
-        round_w2(1, 1)
-        first_products(0, 0, 1)
-        quantise_w2(0, 1)
-        first_products(0, 1, 0)
-        make_h(0, 0, whole)
+        first_products(0, 0, 2)
+        round_w2(0, 1, 256)
         quantise_w2(1, 1)
-        round_regrid(0)
-        first_products(0, 1, 1)
-        quantise_h(0, 0, whole)
+        first_products(0, 1, 0)
+        make_h(0, 0, narrow)
+        first_products(0, 1, 2)
+        quantise_w2(0, 1)
+        quantise_h(0, 0, narrow)
+        make_h(0, 1, narrow)
         first_products(1, 0, 0)
-        make_h(0, 1, whole)
+        quantise_h(0, 1, narrow)
+        first_products(1, 0, 1)
+        round_regrid(0)
+        first_products(1, 0, 2)
+        first_products(1, 0, 3)
         quantise_regrid(0)
         round_regrid(1)
-        first_products(1, 0, 1)
-        quantise_h(0, 1, whole)
-        round_w2(0, 2)
         first_products(1, 1, 0)
-        make_h(1, 0, whole)
-        quantise_regrid(1)
-        round_w2(1, 2)
+        make_h(1, 0, wide)
         first_products(1, 1, 1)
-        quantise_w2(0, 2)
-        quantise_h(1, 0, whole)
-        quantise_w2(1, 2)
+        quantise_regrid(1)
+        quantise_h(1, 0, wide)
+        first_products(1, 1, 2)
         second_product(0, 0)
+        first_products(1, 1, 3)
         second_product(0, 1)
-        first_products(2, 0, 0)
-        make_h(1, 1, whole)
-        first_products(2, 0, 1)
-        quantise_h(1, 1, whole)
-        first_products(2, 1, 0)
+        make_h(1, 1, tiles[0])
+        make_h(1, 1, tiles[1])
+        quantise_h(1, 1, tiles[0])
         second_product(1, 0)
+        make_h(1, 1, tiles[2])
+        quantise_h(1, 1, tiles[1])
         second_product(1, 1)
-        make_h(2, 0, whole)
-        first_products(2, 1, 1)
-        quantise_h(2, 0, whole)
-        make_h(2, 1, halves[0])
-        make_h(2, 1, halves[1])
-        quantise_h(2, 1, halves[0])
-        quantise_h(2, 1, halves[1])
-        second_product(2, 0)
-        second_product(2, 1)
+        make_h(1, 1, tiles[3])
+        quantise_h(1, 1, tiles[2])
+        second_product(1, 2)
+        quantise_h(1, 1, tiles[3])
+        last_second_product(1, 3)

@@ -25,6 +25,7 @@ J_PASSES = S // PASS
 BANK = 512
 CHUNKS = ((0, 256), (256, 512))
 R_TILES = H // P
+RUN = 8
 LIST_COLS = PASS // 16
 
 
@@ -50,6 +51,8 @@ def tile_list_flowline_velocity_regrid_kernel(
         nc.vector.memset(w1_plane[:].rearrange("p a n -> p (a n)").bitcast(I32), 0)
         v_plane = kept([P, K_PASSES * S], U8, "v_plane")
         nc.vector.memset(v_plane[:].bitcast(I32), 0)
+        flow_rows = kept([P, P], F32, "flow_rows")
+        nc.vector.memset(flow_rows[:], 0.0)
         identity = kept([P, P], F32, "identity")
         make_identity(nc, identity[:])
 
@@ -66,28 +69,33 @@ def tile_list_flowline_velocity_regrid_kernel(
 
         def load_regrid(g, tag):
             regrid_raw[g] = kept([P, PACK, M], F32, f"regrid_raw{g}", tag)
-            rows = regrid[g * PASS : (g + 1) * PASS, :]
-            nc.sync.dma_start(regrid_raw[g][:], rows.rearrange("(p t) m -> p t m", t=PACK))
+            rows = regrid[g * PASS : (g + 1) * PASS, :].rearrange("(u t i) m -> t u i m", t=PACK, i=RUN)
+            for t in range(PACK):
+                nc.sync.dma_start(regrid_raw[g][:, t, :], rows[t])
 
         load_words(0)
-        for a in range(K_PASSES):
-            nc.scalar.dma_start(scale_window[:].bitcast(I32)[a:P:8, :], tab_scales[a].bitcast(I32))
-        load_w2(0, 0, 256)
-        load_w2(1, 0, 256)
-        load_w2(1, 256, 256)
-        load_words(1)
-
-        left_cols = kept([P, R_TILES], F32, "left_cols")
-        with nc.allow_non_contiguous_dma(reason="one value of a vector to each partition"):
-            nc.scalar.dma_start(left_cols[:], left.rearrange("(c p) -> p c", p=P))
-        w1_codes = kept([P, K_PASSES, 2 * H], U8, "w1_codes")
-        nc.sync.dma_start(w1_codes[:].bitcast(I32), w1_words.rearrange("a p n -> p a n").bitcast(I32))
-        load_w2(1, 512, 256)
+        nc.sync.dma_start(
+            scale_window[:].bitcast(I32)[0:P:4, :], tab_scales.rearrange("a q n -> q a n").bitcast(I32)
+        )
         for q in range(4):
             nc.gpsimd.dma_start(
                 w1_plane[32 * q : 32 * q + 4, :, :].bitcast(I32),
                 w1_scales[:, 4 * q : 4 * q + 4, :].rearrange("a r n -> r a n").bitcast(I32),
             )
+        load_w2(0, 0, 256)
+        load_w2(1, 0, 256)
+        load_words(1)
+        left_cols = kept([P, R_TILES], F32, "left_cols")
+        with nc.allow_non_contiguous_dma(reason="one value of a vector to each partition"):
+            nc.sync.dma_start(left_cols[:], left.rearrange("(c p) -> p c", p=P))
+        for g in range(J_PASSES):
+            nc.sync.dma_start(
+                flow_rows[g * PACK : (g + 1) * PACK, :].rearrange("t (u i) -> t u i", i=RUN),
+                flow[g * PASS : (g + 1) * PASS].rearrange("(u t i) -> t u i", t=PACK, i=RUN),
+            )
+        load_w2(1, 256, 256)
+        w1_codes = kept([P, K_PASSES, 2 * H], U8, "w1_codes")
+        nc.sync.dma_start(w1_codes[:].bitcast(I32), w1_words.rearrange("a p n -> p a n").bitcast(I32))
 
         left_rows = kept([P, H], F32, "left_rows")
         for first in range(0, R_TILES, 4):
@@ -97,28 +105,27 @@ def tile_list_flowline_velocity_regrid_kernel(
                 column = left_cols[:, first + c : first + c + 1].to_broadcast([P, P])
                 nc.tensor.transpose(spread[:, c * P : (c + 1) * P], column, identity[:])
             nc.scalar.activation(left_rows[:, first * P : (first + count) * P], spread[:, : count * P], ACT.Copy)
-
-        flow_cols = kept([P, J_PASSES, PACK], F32, "flow_cols", "left_cols")
-        nc.sync.dma_start(flow_cols[:], flow.rearrange("(g p t) -> p g t", p=P, t=PACK))
+        turned = psum_ab.tile([P, P], F32, name="bank_a")
+        nc.tensor.transpose(turned[:], flow_rows[:], identity[:])
+        flow_cols = kept([P, J_PASSES * PACK], F32, "flow_cols")
+        nc.scalar.activation(flow_cols[:], turned[:, : J_PASSES * PACK], ACT.Copy)
 
         scale_picked = kept([P, S], U8, "scale_picked")
 
         def gather_scales():
             scale_ordered = kept([P, S], U8, "scale_ordered")
             nc.vector.tensor_copy(scale_picked[:], scale_window[:].indirect(offsets[:]))
-            nc.vector.tensor_copy(
-                scale_ordered[:].rearrange("k (g t p) -> k g t p", g=J_PASSES, t=PACK),
-                scale_picked[:].rearrange("k (g p t) -> k g t p", g=J_PASSES, t=PACK),
-            )
             source = scale_ordered[:].bitcast(I32)
+            nc.vector.tensor_copy(
+                source.rearrange("k (g t u w) -> k g t u w", g=J_PASSES, t=PACK, w=RUN // 4),
+                scale_picked[:].bitcast(I32).rearrange("k (g u t w) -> k g t u w", g=J_PASSES, t=PACK, w=RUN // 4),
+            )
             target = v_plane[:].bitcast(I32)
-            for a in range(K_PASSES):
-                for q in range(4):
-                    queue = nc.gpsimd if q == 0 else nc.sync
-                    queue.dma_start(
-                        target[32 * q : 32 * q + 4, a * S // 4 : (a + 1) * S // 4],
-                        source[32 * q + a : 32 * (q + 1) : 8, :],
-                    )
+            for q in range(4):
+                nc.sync.dma_start(
+                    target[32 * q : 32 * q + 4, :].rearrange("r (a n) -> r a n", a=K_PASSES),
+                    source[32 * q : 32 * (q + 1) : 4, :],
+                )
 
         words_picked = kept([P, K_PASSES, S], U32, "words_picked")
         v_codes = [kept([P, K_PASSES, PACK, P], I32, f"v_codes{g}") for g in range(J_PASSES)]
@@ -133,8 +140,8 @@ def tile_list_flowline_velocity_regrid_kernel(
         def order_words(g):
             picked = words_picked[:, :, g * PASS : (g + 1) * PASS].bitcast(I32)
             nc.vector.tensor_copy(
-                v_codes[g][:].rearrange("k a t (c i) -> k a c t i", i=4),
-                picked.rearrange("k a (c i t) -> k a c t i", i=4, t=PACK),
+                v_codes[g][:].rearrange("k a t (u i) -> k a t u i", i=RUN),
+                picked.rearrange("k a (u t i) -> k a t u i", t=PACK, i=RUN),
             )
 
         def round_and_interleave(grouped, raw):
@@ -147,19 +154,19 @@ def tile_list_flowline_velocity_regrid_kernel(
             nc.vector.quantize_mx(out=codes.bitcast(FP8X4), scales=plane, in_=grouped.rearrange("p n t -> p (n t)"))
 
         w2_grouped, w2_codes, w2_plane = {}, {}, {}
-        for a in range(K_PASSES):
-            for c, (first, width) in enumerate(CHUNKS):
-                w2_grouped[a, c] = kept([P, width, PACK], BF16, f"w2_grouped{a}{c}")
-                w2_codes[a, c] = kept([P, width], U32, f"w2_codes{a}{c}")
-                w2_plane[a, c] = kept([P, width], U8, f"w2_plane{a}{c}")
+        for c, (first, width) in enumerate(CHUNKS):
+            w2_grouped[c] = kept([P, K_PASSES * width, PACK], BF16, f"w2_grouped{c}")
+            w2_codes[c] = kept([P, K_PASSES * width], U32, f"w2_codes{c}")
+            w2_plane[c] = kept([P, K_PASSES * width], U8, f"w2_plane{c}")
 
         def round_w2(a, c, first):
             raw = w2_raw[a, first]
-            start = first - CHUNKS[c][0]
-            round_and_interleave(w2_grouped[a, c][:, start : start + raw.shape[2], :], raw[:])
+            start = a * CHUNKS[c][1] + first - CHUNKS[c][0]
+            round_and_interleave(w2_grouped[c][:, start : start + raw.shape[2], :], raw[:])
 
-        def quantise_w2(a, c):
-            quantise(w2_grouped[a, c][:], w2_codes[a, c][:], w2_plane[a, c][:])
+        def quantise_w2(a, c, count=1):
+            cols = slice(a * CHUNKS[c][1], (a + count) * CHUNKS[c][1])
+            quantise(w2_grouped[c][:, cols, :], w2_codes[c][:, cols], w2_plane[c][:, cols])
 
         regrid_grouped = [kept([P, M, PACK], BF16, f"regrid_grouped{g}") for g in range(J_PASSES)]
         regrid_codes = [kept([P, M], U32, f"regrid_codes{g}") for g in range(J_PASSES)]
@@ -180,48 +187,51 @@ def tile_list_flowline_velocity_regrid_kernel(
                 h_codes[c, g] = kept([P, width], U32, f"h_codes{c}{g}")
                 h_plane[c, g] = kept([P, width], U8, f"h_plane{c}{g}")
 
-        def first_products(c, g, t0):
+        def first_products(c, g, *firsts):
             first, width = CHUNKS[c]
             slots = BANK // width
             step = BANK if width == BANK else P
-            bank_a = psum_ab.tile([P, slots, width], F32, name="bank_a")
-            bank_b = psum_ab.tile([P, slots, width], F32, name="bank_b")
-            for u in range(slots):
-                t = t0 + u
-                j0 = g * PASS + t * P
-                for a in range(K_PASSES):
-                    nc.tensor.matmul_mx(
-                        out=bank_b[:, u, :],
-                        lhsT=v_codes[g][:, a, t, :].bitcast(FP8X4),
-                        lhsT_scale=v_plane[:, a * S + j0 : a * S + j0 + P],
-                        rhs=w2_codes[a, c][:].bitcast(FP8X4),
-                        rhs_scale=w2_plane[a, c][:],
-                        start=(a == 0),
-                        stop=(a == K_PASSES - 1),
-                    )
-                for n0 in range(0, width, step):
-                    r0 = first + n0
-                    for a in range(K_PASSES):
+            bank_a, bank_b = {}, {}
+            for t0 in firsts:
+                bank_a[t0] = psum_ab.tile([P, slots, width], F32, name="bank_a")
+                bank_b[t0] = psum_ab.tile([P, slots, width], F32, name="bank_b")
+            for a in range(K_PASSES):
+                for t0 in firsts:
+                    for u in range(slots):
+                        t = t0 + u
+                        j0 = a * S + g * PASS + t * P
                         nc.tensor.matmul_mx(
-                            out=bank_a[:, u, n0 : n0 + step],
+                            out=bank_b[t0][:, u, :],
                             lhsT=v_codes[g][:, a, t, :].bitcast(FP8X4),
-                            lhsT_scale=v_plane[:, a * S + j0 : a * S + j0 + P],
-                            rhs=w1_codes[:, a, 2 * r0 : 2 * (r0 + step)].bitcast(FP4X4),
-                            rhs_scale=w1_plane[:, a, r0 : r0 + step],
-                            start=(a == 0),
-                            stop=(a == K_PASSES - 1),
+                            lhsT_scale=v_plane[:, j0 : j0 + P],
+                            rhs=w2_codes[c][:, a * width : (a + 1) * width].bitcast(FP8X4),
+                            rhs_scale=w2_plane[c][:, a * width : (a + 1) * width],
+                            start=(a == 0 and u == 0),
+                            stop=(a == K_PASSES - 1 and u == slots - 1),
                         )
-            nc.scalar.activation(size_a[c, g][:, t0 : t0 + slots, :], bank_a[:], ACT.Abs)
-            for u in range(slots):
-                t = t0 + u
-                nc.vector.scalar_tensor_tensor(
-                    out=weighted_b[c, g][:, t, :],
-                    in0=bank_b[:, u, :],
-                    scalar=flow_cols[:, g, t : t + 1],
-                    in1=left_rows[:, first : first + width],
-                    op0=MULT,
-                    op1=MULT,
-                )
+                        for n0 in range(0, width, step):
+                            r0 = first + n0
+                            nc.tensor.matmul_mx(
+                                out=bank_a[t0][:, u, n0 : n0 + step],
+                                lhsT=v_codes[g][:, a, t, :].bitcast(FP8X4),
+                                lhsT_scale=v_plane[:, j0 : j0 + P],
+                                rhs=w1_codes[:, a, 2 * r0 : 2 * (r0 + step)].bitcast(FP4X4),
+                                rhs_scale=w1_plane[:, a, r0 : r0 + step],
+                                start=(a == 0 and u == 0 and n0 == 0),
+                                stop=(a == K_PASSES - 1 and u == slots - 1 and n0 + step == width),
+                            )
+            for t0 in firsts:
+                nc.scalar.activation(size_a[c, g][:, t0 : t0 + slots, :], bank_a[t0][:], ACT.Abs)
+                for u in range(slots):
+                    t = t0 + u
+                    nc.vector.scalar_tensor_tensor(
+                        out=weighted_b[c, g][:, t, :],
+                        in0=bank_b[t0][:, u, :],
+                        scalar=flow_cols[:, g * PACK + t : g * PACK + t + 1],
+                        in1=left_rows[:, first : first + width],
+                        op0=MULT,
+                        op1=MULT,
+                    )
 
         def make_h(c, g, cols):
             nc.vector.tensor_tensor(
@@ -276,30 +286,29 @@ def tile_list_flowline_velocity_regrid_kernel(
         round_w2(1, 1, 256)
         gather_scales()
         load_w2(0, 256, 512, "scale_picked")
-        quantise_w2(0, 0)
-        quantise_w2(1, 0)
+        load_w2(1, 512, 256, "scale_ordered")
+        quantise_w2(0, 0, 2)
         gather_words(1, 0, 1)
         order_words(0)
         gather_words(1, 1, 1)
-        load_regrid(0, "scale_ordered")
-        round_w2(1, 1, 512)
         order_words(1)
-        load_regrid(1, "words_picked")
-        bias_cols = kept([P, R_TILES], F32, "bias_cols", "w2_raw1_512")
-        with nc.allow_non_contiguous_dma(reason="one value of a vector to each partition"):
-            nc.sync.dma_start(bias_cols[:], bias.rearrange("(c p) -> p c", p=P))
+        load_regrid(0, "words_picked")
 
         narrow, wide = slice(0, 256), slice(0, 512)
         tiles = [slice(n * P, (n + 1) * P) for n in range(4)]
 
-        first_products(0, 0, 0)
-        first_products(0, 0, 2)
+        first_products(0, 0, 0, 2)
         round_w2(0, 1, 256)
-        quantise_w2(1, 1)
+        load_regrid(1, "scale_picked")
         first_products(0, 1, 0)
         make_h(0, 0, narrow)
-        first_products(0, 1, 2)
         quantise_w2(0, 1)
+        round_w2(1, 1, 512)
+        bias_cols = kept([P, R_TILES], F32, "bias_cols", "scale_ordered")
+        with nc.allow_non_contiguous_dma(reason="one value of a vector to each partition"):
+            nc.sync.dma_start(bias_cols[:], bias.rearrange("(c p) -> p c", p=P))
+        first_products(0, 1, 2)
+        quantise_w2(1, 1)
         quantise_h(0, 0, narrow)
         make_h(0, 1, narrow)
         first_products(1, 0, 0)

@@ -23,7 +23,7 @@ PASS = P * PACK
 K_PASSES = K // PASS
 J_PASSES = S // PASS
 BANK = 512
-CHUNKS = ((0, 256), (256, 512))
+CHUNKS = ((0, 256), (256, 256), (512, 256))
 R_TILES = H // P
 RUN = 8
 LIST_COLS = PASS // 16
@@ -62,10 +62,13 @@ def tile_list_flowline_velocity_regrid_kernel(
         def load_words(a):
             nc.sync.dma_start(word_window[a][:], tab_words[a].rearrange("p t i -> p (t i)").bitcast(I32))
 
-        def load_w2(a, first, width, tag=None):
-            w2_raw[a, first] = kept([P, PACK, width], F32, f"w2_raw{a}_{first}", tag)
-            rows = w2[a * PASS : (a + 1) * PASS, first : first + width]
-            nc.sync.dma_start(w2_raw[a, first][:], rows.rearrange("(p i) n -> p i n", i=PACK))
+        def load_w2(a, chunks, tag=None):
+            width = CHUNKS[0][1]
+            raw = kept([P, len(chunks), PACK, width], F32, f"w2_raw{a}{chunks[0]}", tag)
+            for n, c in enumerate(chunks):
+                rows = w2[a * PASS : (a + 1) * PASS, c * width : (c + 1) * width]
+                nc.sync.dma_start(raw[:, n, :, :], rows.rearrange("(p i) n -> p i n", i=PACK))
+                w2_raw[a, c] = raw[:, n, :, :]
 
         def load_regrid(g, tag):
             regrid_raw[g] = kept([P, PACK, M], F32, f"regrid_raw{g}", tag)
@@ -82,8 +85,8 @@ def tile_list_flowline_velocity_regrid_kernel(
                 w1_plane[32 * q : 32 * q + 4, :, :].bitcast(I32),
                 w1_scales[:, 4 * q : 4 * q + 4, :].rearrange("a r n -> r a n").bitcast(I32),
             )
-        load_w2(0, 0, 256)
-        load_w2(1, 0, 256)
+        load_w2(0, [0])
+        load_w2(1, [0])
         load_words(1)
         left_cols = kept([P, R_TILES], F32, "left_cols")
         with nc.allow_non_contiguous_dma(reason="one value of a vector to each partition"):
@@ -93,7 +96,7 @@ def tile_list_flowline_velocity_regrid_kernel(
                 flow_rows[g * PACK : (g + 1) * PACK, :].rearrange("t (u i) -> t u i", i=RUN),
                 flow[g * PASS : (g + 1) * PASS].rearrange("(u t i) -> t u i", t=PACK, i=RUN),
             )
-        load_w2(1, 256, 256)
+        load_w2(1, [1])
         w1_codes = kept([P, K_PASSES, 2 * H], U8, "w1_codes")
         nc.sync.dma_start(w1_codes[:].bitcast(I32), w1_words.rearrange("a p n -> p a n").bitcast(I32))
 
@@ -159,10 +162,9 @@ def tile_list_flowline_velocity_regrid_kernel(
             w2_codes[c] = kept([P, K_PASSES * width], U32, f"w2_codes{c}")
             w2_plane[c] = kept([P, K_PASSES * width], U8, f"w2_plane{c}")
 
-        def round_w2(a, c, first):
-            raw = w2_raw[a, first]
-            start = a * CHUNKS[c][1] + first - CHUNKS[c][0]
-            round_and_interleave(w2_grouped[c][:, start : start + raw.shape[2], :], raw[:])
+        def round_w2(a, c):
+            width = CHUNKS[c][1]
+            round_and_interleave(w2_grouped[c][:, a * width : (a + 1) * width, :], w2_raw[a, c])
 
         def quantise_w2(a, c, count=1):
             cols = slice(a * CHUNKS[c][1], (a + count) * CHUNKS[c][1])
@@ -277,66 +279,68 @@ def tile_list_flowline_velocity_regrid_kernel(
             result_high = kept([P, M // 2], F32, "result_high")
             nc.vector.tensor_scalar_add(result_low[:], acc_low[:], bias_cols[:, r_tile : r_tile + 1])
             nc.sync.dma_start(out[rows, low], result_low[:])
-            nc.scalar.activation(result_high[:], acc_high[:], ACT.Identity, bias=bias_cols[:, r_tile : r_tile + 1])
+            nc.vector.tensor_scalar_add(result_high[:], acc_high[:], bias_cols[:, r_tile : r_tile + 1])
             nc.scalar.dma_start(out[rows, high], result_high[:])
 
         gather_words(0, 0, 2)
-        round_w2(0, 0, 0)
-        round_w2(1, 0, 0)
-        round_w2(1, 1, 256)
+        round_w2(0, 0)
+        round_w2(1, 0)
+        round_w2(1, 1)
         gather_scales()
-        load_w2(0, 256, 512, "scale_picked")
-        load_w2(1, 512, 256, "scale_ordered")
+        load_w2(0, [1, 2], "scale_picked")
+        load_w2(1, [2], "scale_ordered")
         quantise_w2(0, 0, 2)
         gather_words(1, 0, 1)
         order_words(0)
         gather_words(1, 1, 1)
         order_words(1)
         load_regrid(0, "words_picked")
+        round_w2(0, 1)
 
-        narrow, wide = slice(0, 256), slice(0, 512)
-        tiles = [slice(n * P, (n + 1) * P) for n in range(4)]
+        whole = slice(0, 256)
+        tiles = [slice(n * P, (n + 1) * P) for n in range(2)]
 
-        first_products(0, 0, 0, 2)
-        round_w2(0, 1, 256)
-        load_regrid(1, "scale_picked")
+        first_products(0, 0, 0)
+        first_products(0, 0, 2)
+        quantise_w2(0, 1, 2)
         first_products(0, 1, 0)
-        make_h(0, 0, narrow)
-        quantise_w2(0, 1)
-        round_w2(1, 1, 512)
+        round_w2(0, 2)
+        load_regrid(1, "scale_picked")
+        make_h(0, 0, whole)
+        first_products(0, 1, 2)
+        round_w2(1, 2)
         bias_cols = kept([P, R_TILES], F32, "bias_cols", "scale_ordered")
         with nc.allow_non_contiguous_dma(reason="one value of a vector to each partition"):
             nc.sync.dma_start(bias_cols[:], bias.rearrange("(c p) -> p c", p=P))
-        first_products(0, 1, 2)
-        quantise_w2(1, 1)
-        quantise_h(0, 0, narrow)
-        make_h(0, 1, narrow)
+        quantise_h(0, 0, whole)
         first_products(1, 0, 0)
-        quantise_h(0, 1, narrow)
-        first_products(1, 0, 1)
-        round_regrid(0)
+        make_h(0, 1, whole)
         first_products(1, 0, 2)
-        first_products(1, 0, 3)
-        quantise_regrid(0)
-        round_regrid(1)
+        round_regrid(0)
+        quantise_h(0, 1, whole)
         first_products(1, 1, 0)
-        make_h(1, 0, wide)
-        first_products(1, 1, 1)
-        quantise_regrid(1)
-        quantise_h(1, 0, wide)
+        make_h(1, 0, whole)
+        quantise_w2(0, 2, 2)
         first_products(1, 1, 2)
+        round_regrid(1)
+        quantise_h(1, 0, whole)
+        first_products(2, 0, 0)
+        make_h(1, 1, whole)
+        quantise_regrid(0)
+        first_products(2, 0, 2)
+        quantise_h(1, 1, whole)
+        quantise_regrid(1)
+        first_products(2, 1, 0)
         second_product(0, 0)
-        first_products(1, 1, 3)
         second_product(0, 1)
-        make_h(1, 1, tiles[0])
-        make_h(1, 1, tiles[1])
-        quantise_h(1, 1, tiles[0])
+        make_h(2, 0, whole)
+        first_products(2, 1, 2)
         second_product(1, 0)
-        make_h(1, 1, tiles[2])
-        quantise_h(1, 1, tiles[1])
         second_product(1, 1)
-        make_h(1, 1, tiles[3])
-        quantise_h(1, 1, tiles[2])
-        second_product(1, 2)
-        quantise_h(1, 1, tiles[3])
-        last_second_product(1, 3)
+        quantise_h(2, 0, whole)
+        make_h(2, 1, tiles[0])
+        make_h(2, 1, tiles[1])
+        quantise_h(2, 1, tiles[0])
+        quantise_h(2, 1, tiles[1])
+        second_product(2, 0)
+        last_second_product(2, 1)

@@ -22,11 +22,15 @@ PACK = 4
 PASS = P * PACK
 K_PASSES = K // PASS
 J_PASSES = S // PASS
-BANK = 512
-CHUNKS = ((0, 256), (256, 256), (512, 256))
-R_TILES = H // P
 RUN = 8
-LIST_COLS = PASS // 16
+QUADRANT = 32
+GROUP = 16
+LIST_COLS = PASS // GROUP
+CHUNK = 256
+CHUNKS = H // CHUNK
+SLOTS_PER_BANK = 2
+R_TILES = H // P
+TILES_PER_BANK = 4
 
 
 def tile_list_flowline_velocity_regrid_kernel(
@@ -39,16 +43,16 @@ def tile_list_flowline_velocity_regrid_kernel(
         psum_ab = ctx.enter_context(tc.psum_pool(name="psum_ab", bufs=3))
         psum_out = ctx.enter_context(tc.psum_pool(name="psum_out", bufs=2))
 
-        def kept(shape, dtype, name, tag=None):
-            return keep.tile(shape, dtype, name=name, tag=tag or name, align_bytes=64)
+        def kept(shape, dtype, name, reuse=None):
+            return keep.tile(shape, dtype, name=name, tag=reuse or name, align_bytes=64)
 
-        offsets = keep.tile([P, S // 16], U16, name="offsets")
+        offsets = keep.tile([P, S // GROUP], U16, name="offsets")
         nc.sync.dma_start(offsets[:], offs)
 
         scale_window = kept([P, T], U8, "scale_window")
         nc.vector.memset(scale_window[:].bitcast(I32), 0)
         w1_plane = kept([P, K_PASSES, H], U8, "w1_plane")
-        nc.vector.memset(w1_plane[:].rearrange("p a n -> p (a n)").bitcast(I32), 0)
+        nc.vector.memset(w1_plane[:].rearrange("p z n -> p (z n)").bitcast(I32), 0)
         v_plane = kept([P, K_PASSES * S], U8, "v_plane")
         nc.vector.memset(v_plane[:].bitcast(I32), 0)
         flow_rows = kept([P, P], F32, "flow_rows")
@@ -56,34 +60,33 @@ def tile_list_flowline_velocity_regrid_kernel(
         identity = kept([P, P], F32, "identity")
         make_identity(nc, identity[:])
 
-        word_window = [kept([P, T], I32, f"word_window{a}") for a in range(K_PASSES)]
+        word_window = [kept([P, T], I32, f"word_window{kp}") for kp in range(K_PASSES)]
         w2_raw, regrid_raw = {}, {}
 
-        def load_words(a):
-            nc.sync.dma_start(word_window[a][:], tab_words[a].rearrange("p t i -> p (t i)").bitcast(I32))
+        def load_words(kp):
+            nc.sync.dma_start(word_window[kp][:], tab_words[kp].rearrange("p t i -> p (t i)").bitcast(I32))
 
-        def load_w2(a, chunks, tag=None):
-            width = CHUNKS[0][1]
-            raw = kept([P, len(chunks), PACK, width], F32, f"w2_raw{a}{chunks[0]}", tag)
+        def load_w2(kp, chunks, reuse=None):
+            raw = kept([P, len(chunks), PACK, CHUNK], F32, f"w2_raw{kp}{chunks[0]}", reuse)
             for n, c in enumerate(chunks):
-                rows = w2[a * PASS : (a + 1) * PASS, c * width : (c + 1) * width]
-                nc.sync.dma_start(raw[:, n, :, :], rows.rearrange("(p i) n -> p i n", i=PACK))
-                w2_raw[a, c] = raw[:, n, :, :]
+                rows = w2[kp * PASS : (kp + 1) * PASS, c * CHUNK : (c + 1) * CHUNK]
+                nc.sync.dma_start(raw[:, n, :, :], rows.rearrange("(p t) n -> p t n", t=PACK))
+                w2_raw[kp, c] = raw[:, n, :, :]
 
-        def load_regrid(g, tag):
-            regrid_raw[g] = kept([P, PACK, M], F32, f"regrid_raw{g}", tag)
+        def load_regrid(g, reuse):
+            regrid_raw[g] = kept([P, PACK, M], F32, f"regrid_raw{g}", reuse)
             rows = regrid[g * PASS : (g + 1) * PASS, :].rearrange("(u t i) m -> t u i m", t=PACK, i=RUN)
             for t in range(PACK):
                 nc.sync.dma_start(regrid_raw[g][:, t, :], rows[t])
 
         load_words(0)
         nc.sync.dma_start(
-            scale_window[:].bitcast(I32)[0:P:4, :], tab_scales.rearrange("a q n -> q a n").bitcast(I32)
+            scale_window[:].bitcast(I32)[0:P:4, :], tab_scales.rearrange("z q n -> q z n").bitcast(I32)
         )
-        for q in range(4):
+        for d in range(P // QUADRANT):
             nc.gpsimd.dma_start(
-                w1_plane[32 * q : 32 * q + 4, :, :].bitcast(I32),
-                w1_scales[:, 4 * q : 4 * q + 4, :].rearrange("a r n -> r a n").bitcast(I32),
+                w1_plane[QUADRANT * d : QUADRANT * d + 4, :, :].bitcast(I32),
+                w1_scales[:, 4 * d : 4 * d + 4, :].rearrange("z r n -> r z n").bitcast(I32),
             )
         load_w2(0, [0])
         load_w2(1, [0])
@@ -98,15 +101,15 @@ def tile_list_flowline_velocity_regrid_kernel(
             )
         load_w2(1, [1])
         w1_codes = kept([P, K_PASSES, 2 * H], U8, "w1_codes")
-        nc.sync.dma_start(w1_codes[:].bitcast(I32), w1_words.rearrange("a p n -> p a n").bitcast(I32))
+        nc.sync.dma_start(w1_codes[:].bitcast(I32), w1_words.rearrange("z p n -> p z n").bitcast(I32))
 
         left_rows = kept([P, H], F32, "left_rows")
-        for first in range(0, R_TILES, 4):
-            count = min(4, R_TILES - first)
+        for first in range(0, R_TILES, TILES_PER_BANK):
+            count = min(TILES_PER_BANK, R_TILES - first)
             spread = psum_out.tile([P, M], F32, name="acc")
-            for c in range(count):
-                column = left_cols[:, first + c : first + c + 1].to_broadcast([P, P])
-                nc.tensor.transpose(spread[:, c * P : (c + 1) * P], column, identity[:])
+            for n in range(count):
+                column = left_cols[:, first + n : first + n + 1].to_broadcast([P, P])
+                nc.tensor.transpose(spread[:, n * P : (n + 1) * P], column, identity[:])
             nc.scalar.activation(left_rows[:, first * P : (first + count) * P], spread[:, : count * P], ACT.Copy)
         turned = psum_ab.tile([P, P], F32, name="bank_a")
         nc.tensor.transpose(turned[:], flow_rows[:], identity[:])
@@ -124,27 +127,27 @@ def tile_list_flowline_velocity_regrid_kernel(
                 scale_picked[:].bitcast(I32).rearrange("k (g u t w) -> k g t u w", g=J_PASSES, t=PACK, w=RUN // 4),
             )
             target = v_plane[:].bitcast(I32)
-            for q in range(4):
+            for d in range(P // QUADRANT):
                 nc.sync.dma_start(
-                    target[32 * q : 32 * q + 4, :].rearrange("r (a n) -> r a n", a=K_PASSES),
-                    source[32 * q : 32 * (q + 1) : 4, :],
+                    target[QUADRANT * d : QUADRANT * d + 4, :].rearrange("r (z n) -> r z n", z=K_PASSES),
+                    source[QUADRANT * d : QUADRANT * (d + 1) : 4, :],
                 )
 
         words_picked = kept([P, K_PASSES, S], U32, "words_picked")
         v_codes = [kept([P, K_PASSES, PACK, P], I32, f"v_codes{g}") for g in range(J_PASSES)]
 
-        def gather_words(a, g, count):
-            window = word_window[a][:].bitcast(U32)
+        def gather_words(kp, j_passes):
+            first, stop = j_passes[0], j_passes[-1] + 1
             nc.vector.tensor_copy(
-                words_picked[:, a, g * PASS : (g + count) * PASS],
-                window.indirect(offsets[:, g * LIST_COLS : (g + count) * LIST_COLS]),
+                words_picked[:, kp, first * PASS : stop * PASS],
+                word_window[kp][:].bitcast(U32).indirect(offsets[:, first * LIST_COLS : stop * LIST_COLS]),
             )
 
         def order_words(g):
             picked = words_picked[:, :, g * PASS : (g + 1) * PASS].bitcast(I32)
             nc.vector.tensor_copy(
-                v_codes[g][:].rearrange("k a t (u i) -> k a t u i", i=RUN),
-                picked.rearrange("k a (u t i) -> k a t u i", t=PACK, i=RUN),
+                v_codes[g][:].rearrange("k z t (u i) -> k z t u i", i=RUN),
+                picked.rearrange("k z (u t i) -> k z t u i", t=PACK, i=RUN),
             )
 
         def round_and_interleave(grouped, raw):
@@ -157,190 +160,182 @@ def tile_list_flowline_velocity_regrid_kernel(
             nc.vector.quantize_mx(out=codes.bitcast(FP8X4), scales=plane, in_=grouped.rearrange("p n t -> p (n t)"))
 
         w2_grouped, w2_codes, w2_plane = {}, {}, {}
-        for c, (first, width) in enumerate(CHUNKS):
-            w2_grouped[c] = kept([P, K_PASSES * width, PACK], BF16, f"w2_grouped{c}")
-            w2_codes[c] = kept([P, K_PASSES * width], U32, f"w2_codes{c}")
-            w2_plane[c] = kept([P, K_PASSES * width], U8, f"w2_plane{c}")
+        for c in range(CHUNKS):
+            w2_grouped[c] = kept([P, K_PASSES * CHUNK, PACK], BF16, f"w2_grouped{c}")
+            w2_codes[c] = kept([P, K_PASSES * CHUNK], U32, f"w2_codes{c}")
+            w2_plane[c] = kept([P, K_PASSES * CHUNK], U8, f"w2_plane{c}")
 
-        def round_w2(a, c):
-            width = CHUNKS[c][1]
-            round_and_interleave(w2_grouped[c][:, a * width : (a + 1) * width, :], w2_raw[a, c])
+        def round_w2(kp, c):
+            round_and_interleave(w2_grouped[c][:, kp * CHUNK : (kp + 1) * CHUNK, :], w2_raw[kp, c])
 
-        def quantise_w2(a, c, count=1):
-            cols = slice(a * CHUNKS[c][1], (a + count) * CHUNKS[c][1])
-            quantise(w2_grouped[c][:, cols, :], w2_codes[c][:, cols], w2_plane[c][:, cols])
+        def quantise_w2(c):
+            quantise(w2_grouped[c][:], w2_codes[c][:], w2_plane[c][:])
 
-        regrid_grouped = [kept([P, M, PACK], BF16, f"regrid_grouped{g}") for g in range(J_PASSES)]
-        regrid_codes = [kept([P, M], U32, f"regrid_codes{g}") for g in range(J_PASSES)]
-        regrid_plane = [kept([P, M], U8, f"regrid_plane{g}") for g in range(J_PASSES)]
+        regrid_grouped = kept([P, J_PASSES * M, PACK], BF16, "regrid_grouped")
+        regrid_codes = kept([P, J_PASSES * M], U32, "regrid_codes")
+        regrid_plane = kept([P, J_PASSES * M], U8, "regrid_plane")
 
-        def round_regrid(g):
-            round_and_interleave(regrid_grouped[g][:], regrid_raw[g][:])
-
-        def quantise_regrid(g):
-            quantise(regrid_grouped[g][:], regrid_codes[g][:], regrid_plane[g][:])
+        def round_regrid(g, half):
+            m0 = half * M // 2
+            round_and_interleave(
+                regrid_grouped[:, g * M + m0 : g * M + m0 + M // 2, :], regrid_raw[g][:, :, m0 : m0 + M // 2]
+            )
 
         size_a, weighted_b, h_grouped, h_codes, h_plane = {}, {}, {}, {}, {}
-        for c, (first, width) in enumerate(CHUNKS):
+        for c in range(CHUNKS):
+            h_grouped[c] = kept([P, J_PASSES * CHUNK, PACK], BF16, f"h_grouped{c}")
+            h_codes[c] = kept([P, J_PASSES * CHUNK], U32, f"h_codes{c}")
+            h_plane[c] = kept([P, J_PASSES * CHUNK], U8, f"h_plane{c}")
             for g in range(J_PASSES):
-                size_a[c, g] = kept([P, PACK, width], F32, f"size_a{c}{g}")
-                weighted_b[c, g] = kept([P, PACK, width], F32, f"weighted_b{c}{g}")
-                h_grouped[c, g] = kept([P, width, PACK], BF16, f"h_grouped{c}{g}")
-                h_codes[c, g] = kept([P, width], U32, f"h_codes{c}{g}")
-                h_plane[c, g] = kept([P, width], U8, f"h_plane{c}{g}")
+                size_a[c, g] = kept([P, PACK, CHUNK], F32, f"size_a{c}{g}")
+                weighted_b[c, g] = kept([P, PACK, CHUNK], F32, f"weighted_b{c}{g}")
 
-        def first_products(c, g, *firsts):
-            first, width = CHUNKS[c]
-            slots = BANK // width
-            step = BANK if width == BANK else P
-            bank_a, bank_b = {}, {}
-            for t0 in firsts:
-                bank_a[t0] = psum_ab.tile([P, slots, width], F32, name="bank_a")
-                bank_b[t0] = psum_ab.tile([P, slots, width], F32, name="bank_b")
-            for a in range(K_PASSES):
-                for t0 in firsts:
-                    for u in range(slots):
-                        t = t0 + u
-                        j0 = a * S + g * PASS + t * P
-                        nc.tensor.matmul_mx(
-                            out=bank_b[t0][:, u, :],
-                            lhsT=v_codes[g][:, a, t, :].bitcast(FP8X4),
-                            lhsT_scale=v_plane[:, j0 : j0 + P],
-                            rhs=w2_codes[c][:, a * width : (a + 1) * width].bitcast(FP8X4),
-                            rhs_scale=w2_plane[c][:, a * width : (a + 1) * width],
-                            start=(a == 0 and u == 0),
-                            stop=(a == K_PASSES - 1 and u == slots - 1),
-                        )
-                        for n0 in range(0, width, step):
-                            r0 = first + n0
-                            nc.tensor.matmul_mx(
-                                out=bank_a[t0][:, u, n0 : n0 + step],
-                                lhsT=v_codes[g][:, a, t, :].bitcast(FP8X4),
-                                lhsT_scale=v_plane[:, j0 : j0 + P],
-                                rhs=w1_codes[:, a, 2 * r0 : 2 * (r0 + step)].bitcast(FP4X4),
-                                rhs_scale=w1_plane[:, a, r0 : r0 + step],
-                                start=(a == 0 and u == 0 and n0 == 0),
-                                stop=(a == K_PASSES - 1 and u == slots - 1 and n0 + step == width),
-                            )
-            for t0 in firsts:
-                nc.scalar.activation(size_a[c, g][:, t0 : t0 + slots, :], bank_a[t0][:], ACT.Abs)
-                for u in range(slots):
-                    t = t0 + u
-                    nc.vector.scalar_tensor_tensor(
-                        out=weighted_b[c, g][:, t, :],
-                        in0=bank_b[t0][:, u, :],
-                        scalar=flow_cols[:, g * PACK + t : g * PACK + t + 1],
-                        in1=left_rows[:, first : first + width],
-                        op0=MULT,
-                        op1=MULT,
-                    )
+        def first_products(c, g, t0):
+            slots = range(t0, t0 + SLOTS_PER_BANK)
+            bank_b = psum_ab.tile([P, SLOTS_PER_BANK, CHUNK], F32, name="bank_b")
+            bank_a = psum_ab.tile([P, SLOTS_PER_BANK, CHUNK], F32, name="bank_a")
 
-        def make_h(c, g, cols):
+            def against_table(acc, t, kp, codes, plane):
+                j0 = kp * S + g * PASS + t * P
+                nc.tensor.matmul_mx(
+                    out=acc,
+                    lhsT=v_codes[g][:, kp, t, :].bitcast(FP8X4),
+                    lhsT_scale=v_plane[:, j0 : j0 + P],
+                    rhs=codes,
+                    rhs_scale=plane,
+                    start=(kp == 0),
+                    stop=(kp == K_PASSES - 1),
+                )
+
+            for t in slots:
+                for kp in range(K_PASSES):
+                    cols = slice(kp * CHUNK, (kp + 1) * CHUNK)
+                    codes = w2_codes[c][:, cols].bitcast(FP8X4)
+                    against_table(bank_b[:, t - t0, :], t, kp, codes, w2_plane[c][:, cols])
+            for t in slots:
+                for n0 in range(0, CHUNK, P):
+                    r0 = c * CHUNK + n0
+                    for kp in range(K_PASSES):
+                        codes = w1_codes[:, kp, 2 * r0 : 2 * (r0 + P)].bitcast(FP4X4)
+                        against_table(bank_a[:, t - t0, n0 : n0 + P], t, kp, codes, w1_plane[:, kp, r0 : r0 + P])
+            nc.scalar.activation(size_a[c, g][:, t0 : t0 + SLOTS_PER_BANK, :], bank_a[:], ACT.Abs)
+            for t in slots:
+                nc.vector.scalar_tensor_tensor(
+                    out=weighted_b[c, g][:, t, :],
+                    in0=bank_b[:, t - t0, :],
+                    scalar=flow_cols[:, g * PACK + t : g * PACK + t + 1],
+                    in1=left_rows[:, c * CHUNK : (c + 1) * CHUNK],
+                    op0=MULT,
+                    op1=MULT,
+                )
+
+        def make_h(c, g, n0=0, width=CHUNK):
+            walk = "p t (c i) -> p c t i"
             nc.vector.tensor_tensor(
-                h_grouped[c, g][:, cols, :].rearrange("p (c i) t -> p c t i", i=2),
-                weighted_b[c, g][:, :, cols].rearrange("p t (c i) -> p c t i", i=2),
-                size_a[c, g][:, :, cols].rearrange("p t (c i) -> p c t i", i=2),
+                h_grouped[c][:, g * CHUNK + n0 : g * CHUNK + n0 + width, :].rearrange("p (c i) t -> p c t i", i=2),
+                weighted_b[c, g][:, :, n0 : n0 + width].rearrange(walk, i=2),
+                size_a[c, g][:, :, n0 : n0 + width].rearrange(walk, i=2),
                 MULT,
             )
 
-        def quantise_h(c, g, cols):
-            quantise(h_grouped[c, g][:, cols, :], h_codes[c, g][:, cols], h_plane[c, g][:, cols])
+        def quantise_h(c, first=0, width=J_PASSES * CHUNK):
+            cols = slice(first, first + width)
+            quantise(h_grouped[c][:, cols, :], h_codes[c][:, cols], h_plane[c][:, cols])
 
-        def regrid_product(c, n, acc, m_cols):
-            cols = slice(n * P, (n + 1) * P)
+        def regrid_product(r_tile, acc, m0, width):
+            c, n0 = divmod(r_tile * P, CHUNK)
             for g in range(J_PASSES):
+                cols = slice(g * CHUNK + n0, g * CHUNK + n0 + P)
+                moving = slice(g * M + m0, g * M + m0 + width)
                 nc.tensor.matmul_mx(
                     out=acc,
-                    lhsT=h_codes[c, g][:, cols].bitcast(FP8X4),
-                    lhsT_scale=h_plane[c, g][:, cols],
-                    rhs=regrid_codes[g][:, m_cols].bitcast(FP8X4),
-                    rhs_scale=regrid_plane[g][:, m_cols],
+                    lhsT=h_codes[c][:, cols].bitcast(FP8X4),
+                    lhsT_scale=h_plane[c][:, cols],
+                    rhs=regrid_codes[:, moving].bitcast(FP8X4),
+                    rhs_scale=regrid_plane[:, moving],
                     start=(g == 0),
                     stop=(g == J_PASSES - 1),
                 )
 
-        def second_product(c, n):
-            r_tile = CHUNKS[c][0] // P + n
+        def output_tile(r_tile):
             acc = psum_out.tile([P, M], F32, name="acc")
-            regrid_product(c, n, acc[:], slice(0, M))
+            regrid_product(r_tile, acc[:], 0, M)
             result = ring.tile([P, M], F32, name="result")
             nc.scalar.activation(result[:], acc[:], ACT.Identity, bias=bias_cols[:, r_tile : r_tile + 1])
             nc.sync.dma_start(out[r_tile * P : (r_tile + 1) * P, :], result[:])
 
-        def last_second_product(c, n):
-            r_tile = CHUNKS[c][0] // P + n
+        def last_output_tile(r_tile):
             rows = slice(r_tile * P, (r_tile + 1) * P)
-            low, high = slice(0, M // 2), slice(M // 2, M)
-            acc_low = psum_ab.tile([P, M // 2], F32, name="bank_a")
-            acc_high = psum_ab.tile([P, M // 2], F32, name="bank_b")
-            regrid_product(c, n, acc_low[:], low)
-            regrid_product(c, n, acc_high[:], high)
-            result_low = kept([P, M // 2], F32, "result_low")
-            result_high = kept([P, M // 2], F32, "result_high")
+            half = M // 2
+            acc_low = psum_ab.tile([P, half], F32, name="bank_a")
+            acc_high = psum_ab.tile([P, half], F32, name="bank_b")
+            regrid_product(r_tile, acc_low[:], 0, half)
+            regrid_product(r_tile, acc_high[:], half, half)
+            result_low = kept([P, half], F32, "result_low")
+            result_high = kept([P, half], F32, "result_high")
             nc.vector.tensor_scalar_add(result_low[:], acc_low[:], bias_cols[:, r_tile : r_tile + 1])
-            nc.sync.dma_start(out[rows, low], result_low[:])
+            nc.sync.dma_start(out[rows, :half], result_low[:])
             nc.vector.tensor_scalar_add(result_high[:], acc_high[:], bias_cols[:, r_tile : r_tile + 1])
-            nc.scalar.dma_start(out[rows, high], result_high[:])
+            nc.scalar.dma_start(out[rows, half:], result_high[:])
 
-        gather_words(0, 0, 2)
+        gather_words(0, [0, 1])
         round_w2(0, 0)
         round_w2(1, 0)
         round_w2(1, 1)
         gather_scales()
-        load_w2(0, [1, 2], "scale_picked")
-        load_w2(1, [2], "scale_ordered")
-        quantise_w2(0, 0, 2)
-        gather_words(1, 0, 1)
+        load_w2(0, [1, 2], reuse="scale_picked")
+        load_w2(1, [2], reuse="scale_ordered")
+        quantise_w2(0)
+        gather_words(1, [0])
         order_words(0)
-        gather_words(1, 1, 1)
+        gather_words(1, [1])
         order_words(1)
-        load_regrid(0, "words_picked")
+        load_regrid(0, reuse="words_picked")
         round_w2(0, 1)
-
-        whole = slice(0, 256)
-        tiles = [slice(n * P, (n + 1) * P) for n in range(2)]
 
         first_products(0, 0, 0)
         first_products(0, 0, 2)
-        quantise_w2(0, 1, 2)
+        quantise_w2(1)
         first_products(0, 1, 0)
         round_w2(0, 2)
-        load_regrid(1, "scale_picked")
-        make_h(0, 0, whole)
+        load_regrid(1, reuse="scale_picked")
+        make_h(0, 0)
         first_products(0, 1, 2)
         round_w2(1, 2)
-        bias_cols = kept([P, R_TILES], F32, "bias_cols", "scale_ordered")
+        bias_cols = kept([P, R_TILES], F32, "bias_cols", reuse="scale_ordered")
         with nc.allow_non_contiguous_dma(reason="one value of a vector to each partition"):
             nc.sync.dma_start(bias_cols[:], bias.rearrange("(c p) -> p c", p=P))
-        quantise_h(0, 0, whole)
+
         first_products(1, 0, 0)
-        make_h(0, 1, whole)
+        make_h(0, 1)
+        round_regrid(0, 0)
         first_products(1, 0, 2)
-        round_regrid(0)
-        quantise_h(0, 1, whole)
+        round_regrid(0, 1)
+        quantise_w2(2)
+        quantise_h(0)
         first_products(1, 1, 0)
-        make_h(1, 0, whole)
-        quantise_w2(0, 2, 2)
+        round_regrid(1, 0)
+        make_h(1, 0)
         first_products(1, 1, 2)
-        round_regrid(1)
-        quantise_h(1, 0, whole)
+        round_regrid(1, 1)
+
         first_products(2, 0, 0)
-        make_h(1, 1, whole)
-        quantise_regrid(0)
+        make_h(1, 1)
+        quantise(regrid_grouped[:], regrid_codes[:], regrid_plane[:])
         first_products(2, 0, 2)
-        quantise_h(1, 1, whole)
-        quantise_regrid(1)
+        output_tile(0)
+        output_tile(1)
+        quantise_h(1)
         first_products(2, 1, 0)
-        second_product(0, 0)
-        second_product(0, 1)
-        make_h(2, 0, whole)
+        make_h(2, 0)
         first_products(2, 1, 2)
-        second_product(1, 0)
-        second_product(1, 1)
-        quantise_h(2, 0, whole)
-        make_h(2, 1, tiles[0])
-        make_h(2, 1, tiles[1])
-        quantise_h(2, 1, tiles[0])
-        quantise_h(2, 1, tiles[1])
-        second_product(2, 0)
-        last_second_product(2, 1)
+        output_tile(2)
+        output_tile(3)
+
+        quantise_h(2, 0, CHUNK)
+        make_h(2, 1, 0, P)
+        make_h(2, 1, P, P)
+        quantise_h(2, CHUNK, P)
+        quantise_h(2, CHUNK + P, P)
+        output_tile(4)
+        last_output_tile(5)

from contextlib import ExitStack

import concourse.mybir as mybir
from concourse.masks import make_identity

K, T, S, H, M = 1024, 2048, 1024, 768, 512
FLOPS = 2 * 2 * K * S * H + 2 * S * H * M

F32 = mybir.dt.float32
BF16 = mybir.dt.bfloat16
I32 = mybir.dt.int32
U32 = mybir.dt.uint32
U16 = mybir.dt.uint16
U8 = mybir.dt.uint8
FP8X4 = mybir.dt.float8_e4m3fn_x4
FP4X4 = mybir.dt.float4_e2m1fn_x4
MULT = mybir.AluOpType.mult
ACT = mybir.ActivationFunctionType

P = 128
PACK = 4
PASS = P * PACK
K_PASSES = K // PASS
J_PASSES = S // PASS
RUN = 8
QUADRANT = 32
GROUP = 16
LIST_COLS = PASS // GROUP
CHUNK = 256
CHUNKS = H // CHUNK
SLOTS_PER_BANK = 2
R_TILES = H // P
TILES_PER_BANK = 4


def tile_list_flowline_velocity_regrid_kernel(
    tc, tab_words, tab_scales, offs, w1_words, w1_scales, w2, left, flow, regrid, bias, out
):
    nc = tc.nc
    with ExitStack() as ctx:
        keep = ctx.enter_context(tc.tile_pool(name="keep", bufs=1))
        ring = ctx.enter_context(tc.tile_pool(name="ring", bufs=3))
        psum_ab = ctx.enter_context(tc.psum_pool(name="psum_ab", bufs=3))
        psum_out = ctx.enter_context(tc.psum_pool(name="psum_out", bufs=2))

        def kept(shape, dtype, name, reuse=None):
            return keep.tile(shape, dtype, name=name, tag=reuse or name, align_bytes=64)

        offsets = keep.tile([P, S // GROUP], U16, name="offsets")
        nc.sync.dma_start(offsets[:], offs)

        scale_window = kept([P, T], U8, "scale_window")
        nc.vector.memset(scale_window[:].bitcast(I32), 0)
        w1_plane = kept([P, K_PASSES, H], U8, "w1_plane")
        nc.vector.memset(w1_plane[:].rearrange("p z n -> p (z n)").bitcast(I32), 0)
        v_plane = kept([P, K_PASSES * S], U8, "v_plane")
        nc.vector.memset(v_plane[:].bitcast(I32), 0)
        flow_rows = kept([P, P], F32, "flow_rows")
        nc.vector.memset(flow_rows[:], 0.0)
        identity = kept([P, P], F32, "identity")
        make_identity(nc, identity[:])

        word_window = [kept([P, T], I32, f"word_window{kp}") for kp in range(K_PASSES)]
        w2_raw, regrid_raw = {}, {}

        def load_words(kp):
            nc.sync.dma_start(word_window[kp][:], tab_words[kp].rearrange("p t i -> p (t i)").bitcast(I32))

        def load_w2(kp, chunks, reuse=None):
            raw = kept([P, len(chunks), PACK, CHUNK], F32, f"w2_raw{kp}{chunks[0]}", reuse)
            for n, c in enumerate(chunks):
                rows = w2[kp * PASS : (kp + 1) * PASS, c * CHUNK : (c + 1) * CHUNK]
                nc.sync.dma_start(raw[:, n, :, :], rows.rearrange("(p t) n -> p t n", t=PACK))
                w2_raw[kp, c] = raw[:, n, :, :]

        def load_regrid(g, reuse):
            regrid_raw[g] = kept([P, PACK, M], F32, f"regrid_raw{g}", reuse)
            rows = regrid[g * PASS : (g + 1) * PASS, :].rearrange("(u t i) m -> t u i m", t=PACK, i=RUN)
            for t in range(PACK):
                nc.sync.dma_start(regrid_raw[g][:, t, :], rows[t])

        load_words(0)
        nc.sync.dma_start(
            scale_window[:].bitcast(I32)[0:P:4, :], tab_scales.rearrange("z q n -> q z n").bitcast(I32)
        )
        for d in range(P // QUADRANT):
            nc.gpsimd.dma_start(
                w1_plane[QUADRANT * d : QUADRANT * d + 4, :, :].bitcast(I32),
                w1_scales[:, 4 * d : 4 * d + 4, :].rearrange("z r n -> r z n").bitcast(I32),
            )
        load_w2(0, [0])
        load_w2(1, [0])
        load_words(1)
        left_cols = kept([P, R_TILES], F32, "left_cols")
        with nc.allow_non_contiguous_dma(reason="one value of a vector to each partition"):
            nc.sync.dma_start(left_cols[:], left.rearrange("(c p) -> p c", p=P))
        for g in range(J_PASSES):
            nc.sync.dma_start(
                flow_rows[g * PACK : (g + 1) * PACK, :].rearrange("t (u i) -> t u i", i=RUN),
                flow[g * PASS : (g + 1) * PASS].rearrange("(u t i) -> t u i", t=PACK, i=RUN),
            )
        load_w2(1, [1])
        w1_codes = kept([P, K_PASSES, 2 * H], U8, "w1_codes")
        nc.sync.dma_start(w1_codes[:].bitcast(I32), w1_words.rearrange("z p n -> p z n").bitcast(I32))

        left_rows = kept([P, H], F32, "left_rows")
        for first in range(0, R_TILES, TILES_PER_BANK):
            count = min(TILES_PER_BANK, R_TILES - first)
            spread = psum_out.tile([P, M], F32, name="acc")
            for n in range(count):
                column = left_cols[:, first + n : first + n + 1].to_broadcast([P, P])
                nc.tensor.transpose(spread[:, n * P : (n + 1) * P], column, identity[:])
            nc.scalar.activation(left_rows[:, first * P : (first + count) * P], spread[:, : count * P], ACT.Copy)
        turned = psum_ab.tile([P, P], F32, name="bank_a")
        nc.tensor.transpose(turned[:], flow_rows[:], identity[:])
        flow_cols = kept([P, J_PASSES * PACK], F32, "flow_cols")
        nc.scalar.activation(flow_cols[:], turned[:, : J_PASSES * PACK], ACT.Copy)

        scale_picked = kept([P, S], U8, "scale_picked")

        def gather_scales():
            scale_ordered = kept([P, S], U8, "scale_ordered")
            nc.vector.tensor_copy(scale_picked[:], scale_window[:].indirect(offsets[:]))
            source = scale_ordered[:].bitcast(I32)
            nc.vector.tensor_copy(
                source.rearrange("k (g t u w) -> k g t u w", g=J_PASSES, t=PACK, w=RUN // 4),
                scale_picked[:].bitcast(I32).rearrange("k (g u t w) -> k g t u w", g=J_PASSES, t=PACK, w=RUN // 4),
            )
            target = v_plane[:].bitcast(I32)
            for d in range(P // QUADRANT):
                nc.sync.dma_start(
                    target[QUADRANT * d : QUADRANT * d + 4, :].rearrange("r (z n) -> r z n", z=K_PASSES),
                    source[QUADRANT * d : QUADRANT * (d + 1) : 4, :],
                )

        words_picked = kept([P, K_PASSES, S], U32, "words_picked")
        v_codes = [kept([P, K_PASSES, PACK, P], I32, f"v_codes{g}") for g in range(J_PASSES)]

        def gather_words(kp, j_passes):
            first, stop = j_passes[0], j_passes[-1] + 1
            nc.vector.tensor_copy(
                words_picked[:, kp, first * PASS : stop * PASS],
                word_window[kp][:].bitcast(U32).indirect(offsets[:, first * LIST_COLS : stop * LIST_COLS]),
            )

        def order_words(g):
            picked = words_picked[:, :, g * PASS : (g + 1) * PASS].bitcast(I32)
            nc.vector.tensor_copy(
                v_codes[g][:].rearrange("k z t (u i) -> k z t u i", i=RUN),
                picked.rearrange("k z (u t i) -> k z t u i", t=PACK, i=RUN),
            )

        def round_and_interleave(grouped, raw):
            nc.scalar.copy(
                grouped.rearrange("p (c i) t -> p c t i", i=4),
                raw.rearrange("p t (c i) -> p c t i", i=4),
            )

        def quantise(grouped, codes, plane):
            nc.vector.quantize_mx(out=codes.bitcast(FP8X4), scales=plane, in_=grouped.rearrange("p n t -> p (n t)"))

        w2_grouped, w2_codes, w2_plane = {}, {}, {}
        for c in range(CHUNKS):
            w2_grouped[c] = kept([P, K_PASSES * CHUNK, PACK], BF16, f"w2_grouped{c}")
            w2_codes[c] = kept([P, K_PASSES * CHUNK], U32, f"w2_codes{c}")
            w2_plane[c] = kept([P, K_PASSES * CHUNK], U8, f"w2_plane{c}")

        def round_w2(kp, c):
            round_and_interleave(w2_grouped[c][:, kp * CHUNK : (kp + 1) * CHUNK, :], w2_raw[kp, c])

        def quantise_w2(c):
            quantise(w2_grouped[c][:], w2_codes[c][:], w2_plane[c][:])

        regrid_grouped = kept([P, J_PASSES * M, PACK], BF16, "regrid_grouped")
        regrid_codes = kept([P, J_PASSES * M], U32, "regrid_codes")
        regrid_plane = kept([P, J_PASSES * M], U8, "regrid_plane")

        def round_regrid(g, half):
            m0 = half * M // 2
            round_and_interleave(
                regrid_grouped[:, g * M + m0 : g * M + m0 + M // 2, :], regrid_raw[g][:, :, m0 : m0 + M // 2]
            )

        size_a, weighted_b, h_grouped, h_codes, h_plane = {}, {}, {}, {}, {}
        for c in range(CHUNKS):
            h_grouped[c] = kept([P, J_PASSES * CHUNK, PACK], BF16, f"h_grouped{c}")
            h_codes[c] = kept([P, J_PASSES * CHUNK], U32, f"h_codes{c}")
            h_plane[c] = kept([P, J_PASSES * CHUNK], U8, f"h_plane{c}")
            for g in range(J_PASSES):
                size_a[c, g] = kept([P, PACK, CHUNK], F32, f"size_a{c}{g}")
                weighted_b[c, g] = kept([P, PACK, CHUNK], F32, f"weighted_b{c}{g}")

        def first_products(c, g, t0):
            slots = range(t0, t0 + SLOTS_PER_BANK)
            bank_b = psum_ab.tile([P, SLOTS_PER_BANK, CHUNK], F32, name="bank_b")
            bank_a = psum_ab.tile([P, SLOTS_PER_BANK, CHUNK], F32, name="bank_a")

            def against_table(acc, t, kp, codes, plane):
                j0 = kp * S + g * PASS + t * P
                nc.tensor.matmul_mx(
                    out=acc,
                    lhsT=v_codes[g][:, kp, t, :].bitcast(FP8X4),
                    lhsT_scale=v_plane[:, j0 : j0 + P],
                    rhs=codes,
                    rhs_scale=plane,
                    start=(kp == 0),
                    stop=(kp == K_PASSES - 1),
                )

            for t in slots:
                for kp in range(K_PASSES):
                    cols = slice(kp * CHUNK, (kp + 1) * CHUNK)
                    codes = w2_codes[c][:, cols].bitcast(FP8X4)
                    against_table(bank_b[:, t - t0, :], t, kp, codes, w2_plane[c][:, cols])
            for t in slots:
                for n0 in range(0, CHUNK, P):
                    r0 = c * CHUNK + n0
                    for kp in range(K_PASSES):
                        codes = w1_codes[:, kp, 2 * r0 : 2 * (r0 + P)].bitcast(FP4X4)
                        against_table(bank_a[:, t - t0, n0 : n0 + P], t, kp, codes, w1_plane[:, kp, r0 : r0 + P])
            nc.scalar.activation(size_a[c, g][:, t0 : t0 + SLOTS_PER_BANK, :], bank_a[:], ACT.Abs)
            for t in slots:
                nc.vector.scalar_tensor_tensor(
                    out=weighted_b[c, g][:, t, :],
                    in0=bank_b[:, t - t0, :],
                    scalar=flow_cols[:, g * PACK + t : g * PACK + t + 1],
                    in1=left_rows[:, c * CHUNK : (c + 1) * CHUNK],
                    op0=MULT,
                    op1=MULT,
                )

        def make_h(c, g, n0=0, width=CHUNK):
            walk = "p t (c i) -> p c t i"
            nc.vector.tensor_tensor(
                h_grouped[c][:, g * CHUNK + n0 : g * CHUNK + n0 + width, :].rearrange("p (c i) t -> p c t i", i=2),
                weighted_b[c, g][:, :, n0 : n0 + width].rearrange(walk, i=2),
                size_a[c, g][:, :, n0 : n0 + width].rearrange(walk, i=2),
                MULT,
            )

        def quantise_h(c, first=0, width=J_PASSES * CHUNK):
            cols = slice(first, first + width)
            quantise(h_grouped[c][:, cols, :], h_codes[c][:, cols], h_plane[c][:, cols])

        def regrid_product(r_tile, acc, m0, width):
            c, n0 = divmod(r_tile * P, CHUNK)
            for g in range(J_PASSES):
                cols = slice(g * CHUNK + n0, g * CHUNK + n0 + P)
                moving = slice(g * M + m0, g * M + m0 + width)
                nc.tensor.matmul_mx(
                    out=acc,
                    lhsT=h_codes[c][:, cols].bitcast(FP8X4),
                    lhsT_scale=h_plane[c][:, cols],
                    rhs=regrid_codes[:, moving].bitcast(FP8X4),
                    rhs_scale=regrid_plane[:, moving],
                    start=(g == 0),
                    stop=(g == J_PASSES - 1),
                )

        def output_tile(r_tile):
            acc = psum_out.tile([P, M], F32, name="acc")
            regrid_product(r_tile, acc[:], 0, M)
            result = ring.tile([P, M], F32, name="result")
            nc.scalar.activation(result[:], acc[:], ACT.Identity, bias=bias_cols[:, r_tile : r_tile + 1])
            nc.sync.dma_start(out[r_tile * P : (r_tile + 1) * P, :], result[:])

        def last_output_tile(r_tile):
            rows = slice(r_tile * P, (r_tile + 1) * P)
            half = M // 2
            acc_low = psum_ab.tile([P, half], F32, name="bank_a")
            acc_high = psum_ab.tile([P, half], F32, name="bank_b")
            regrid_product(r_tile, acc_low[:], 0, half)
            regrid_product(r_tile, acc_high[:], half, half)
            result_low = kept([P, half], F32, "result_low")
            result_high = kept([P, half], F32, "result_high")
            nc.vector.tensor_scalar_add(result_low[:], acc_low[:], bias_cols[:, r_tile : r_tile + 1])
            nc.sync.dma_start(out[rows, :half], result_low[:])
            nc.vector.tensor_scalar_add(result_high[:], acc_high[:], bias_cols[:, r_tile : r_tile + 1])
            nc.scalar.dma_start(out[rows, half:], result_high[:])

        gather_words(0, [0, 1])
        round_w2(0, 0)
        round_w2(1, 0)
        round_w2(1, 1)
        gather_scales()
        load_w2(0, [1, 2], reuse="scale_picked")
        load_w2(1, [2], reuse="scale_ordered")
        quantise_w2(0)
        gather_words(1, [0])
        order_words(0)
        gather_words(1, [1])
        order_words(1)
        load_regrid(0, reuse="words_picked")
        round_w2(0, 1)

        first_products(0, 0, 0)
        first_products(0, 0, 2)
        quantise_w2(1)
        first_products(0, 1, 0)
        round_w2(0, 2)
        load_regrid(1, reuse="scale_picked")
        make_h(0, 0)
        first_products(0, 1, 2)
        round_w2(1, 2)
        bias_cols = kept([P, R_TILES], F32, "bias_cols", reuse="scale_ordered")
        with nc.allow_non_contiguous_dma(reason="one value of a vector to each partition"):
            nc.sync.dma_start(bias_cols[:], bias.rearrange("(c p) -> p c", p=P))

        first_products(1, 0, 0)
        make_h(0, 1)
        round_regrid(0, 0)
        first_products(1, 0, 2)
        round_regrid(0, 1)
        quantise_w2(2)
        quantise_h(0)
        first_products(1, 1, 0)
        round_regrid(1, 0)
        make_h(1, 0)
        first_products(1, 1, 2)
        round_regrid(1, 1)

        first_products(2, 0, 0)
        make_h(1, 1)
        quantise(regrid_grouped[:], regrid_codes[:], regrid_plane[:])
        first_products(2, 0, 2)
        output_tile(0)
        output_tile(1)
        quantise_h(1)
        first_products(2, 1, 0)
        make_h(2, 0)
        first_products(2, 1, 2)
        output_tile(2)
        output_tile(3)

        quantise_h(2, 0, CHUNK)
        make_h(2, 1, 0, P)
        make_h(2, 1, P, P)
        quantise_h(2, CHUNK, P)
        quantise_h(2, CHUNK + P, P)
        output_tile(4)
        last_output_tile(5)
